import numpy as np, ml_dtypes
CORES = [2,3,42,43,82,83,122,123]
N = 8
BF = ml_dtypes.bfloat16
def gentries(a):
    return np.ascontiguousarray(a.reshape(8, 16, -1).transpose(0, 2, 1)).reshape(8, -1)
def gtable(e):
    e = np.asarray(e); return np.ascontiguousarray(e.reshape(8, -1, 16).transpose(0, 2, 1)).reshape(128, -1).astype(np.int32)
M, L, S, ST = 384, 3, 1024, 8
LPR, C, W = 2, 1186, 9504
LEV = [(16, LPR, 0), (32, 16 * LPR, LPR)] + [(288 + d * N * M, M, 17 * LPR + d * M) for d in range(L)]
START = np.array([v[0] for v in LEV]); SIZE = np.array([v[1] for v in LEV])
A8 = np.arange(8)[:, None]
def grow(rng, bias):
    tri = np.zeros((N, 8, 16, C), np.int64); par = np.zeros((N, 8, C - LPR), np.int64); let = np.zeros((N, 8, C - LPR), np.int64)
    G = np.zeros((8, 16, W), np.int64); G[:, :, 0] = 16 + np.arange(16)
    D = [np.repeat(G[:, :, :1], LPR, axis=2) for r in range(N)]
    for d in range(len(LEV)):
        b, m, o = LEV[d]; new = []
        for r in range(N):
            own = tri[r, :, :, o:o + m]
            if d + 1 < len(LEV):
                b2, m2, o2 = LEV[d + 1]
                n = D[r].transpose(0, 2, 1); lev = np.searchsorted(START, n, side="right"); who = (n - START[lev - 1]) // SIZE[lev - 1]
                key = rng.random((8, m, 16)) + bias(d, r, lev, who)
                pick = rng.permuted(np.argsort(key.reshape(8, -1), axis=1)[:, :m2], axis=1)
                p = pick >> 4; c = pick & 15
                par[r, :, o2 - LPR:o2 - LPR + m2] = p; let[r, :, o2 - LPR:o2 - LPR + m2] = c
                own[A8, c, p] = b2 + r * m2 + np.arange(m2)
                new.append(D[r][A8, c, p])
            G[:, :, b + r * m:b + (r + 1) * m] = np.where(own != 0, own, D[r])
        D = [np.take_along_axis(G, fl[:, None, :], 2) for fl in new]
    return tri, par, let, G
def walk(rng, G, go):
    txt = np.zeros((N, 8, ST, S), np.int64); s = np.zeros((N, 8, S), np.int64)
    for t in range(ST):
        col = G[np.arange(8)[None, :, None], :, s]
        c = np.argmax(rng.random(col.shape) + (col > s[..., None]) * (rng.random((N, 8, S, 1)) < go[..., None]), axis=-1)
        txt[:, :, t] = c; s = np.take_along_axis(col, c[..., None], 3)[..., 0]
    return txt
def pack(tri, par, let, txt):
    return {"tri": np.ascontiguousarray(tri.reshape(N, 128, C)).astype(np.int32), "par": np.stack([gtable(a) for a in par]),
            "let": let.astype(np.int32), "txt": np.ascontiguousarray(txt.reshape(N, 8, ST * S)).astype(np.int32)}
def setup_inputs(rng):
    pull = rng.choice(np.array([0.0, 0.2, 0.5, 2.0]), (N, 8, 1, 1))
    tri, par, let, G = grow(rng, lambda d, r, lev, who: -pull[r] * lev)
    return pack(tri, par, let, walk(rng, G, rng.choice(np.array([0.3, 0.7, 0.95]), (N, 8, S))))
def setup_inputs_depth(rng):
    pull = np.where(rng.permutation(8) < 4, 4.0, -4.0).reshape(8, 1, 1)
    tri, par, let, G = grow(rng, lambda d, r, lev, who: -pull * lev)
    return pack(tri, par, let, walk(rng, G, rng.choice(np.array([0.5, 1.0, 1.0]), (N, 8, S))))
def setup_inputs_bushy(rng):
    def bias(d, r, lev, who):
        v = np.zeros(lev.shape); m = lev.shape[1]
        v[0::2] = 10.0 * np.argsort(rng.random((4, m)), axis=1)[:, :, None]
        v[1::2] = 10.0 * np.argsort(rng.random((4, m, 16)), axis=2)
        return v
    tri, par, let, G = grow(rng, bias)
    txt = walk(rng, G, rng.choice(np.array([0.2, 0.8, 1.0]), (N, 8, S)))
    for r in range(N):
        g = 2 * rng.permutation(4) + 1
        txt[r, g[0]] = (np.add.accumulate(rng.integers(1, 16, ST)) & 15)[:, None]
        txt[r, g[1]] = LPR * ((r + 1 + int(rng.integers(0, N - 1))) % N) + rng.integers(0, LPR, (ST, S))
    return pack(tri, par, let, txt)
def setup_inputs_ends(rng):
    def bias(d, r, lev, who):
        v = np.zeros(lev.shape); m = lev.shape[1]; p = np.arange(m); c = np.arange(16)
        v[0::2] = 100.0 * np.minimum(p, m - 1 - p)[None, :, None]
        v[1::2] = 10.0 * ((c != 0) & (c != 15))[None, None, :] - 0.5 * lev[1::2]
        return v
    tri, par, let, G = grow(rng, bias)
    txt = walk(rng, G, rng.choice(np.array([0.3, 0.7, 1.0]), (N, 8, S))); q = S >> 3
    txt[..., :q] = 0; txt[..., q:2 * q] = 15
    txt[..., 2 * q:3 * q] = (15 * (np.arange(ST) & 1))[None, None, :, None]
    txt[..., 3 * q:4 * q] = rng.integers(0, 16, (N, 8, 1, q)); txt[..., 4 * q:5 * q] = txt[..., 7 * q:7 * q + 1]
    return pack(tri, par, let, txt)
def setup_inputs_spread(rng):
    wt = np.stack([0.15 * rng.permutation(16) ** np.exp2(rng.integers(-1, 2)) for g in range(8)])[:, None, :]
    pull = rng.choice(np.array([-0.5, 0.0, 0.5, 3.0]), (len(LEV), N, 8, 1, 1)); q = int(rng.integers(0, N))
    tri, par, let, G = grow(rng, lambda d, r, lev, who: wt - pull[d, r] * lev + (100.0 if d == 2 else 0.0) * (who != q))
    txt = walk(rng, G, rng.random((N, 8, S)))
    odd = np.minimum((16 * rng.random((N, 8, ST, S)) ** np.exp2(rng.integers(-3, 4, (N, 8, 1, S)))).astype(np.int64), 15)
    return pack(tri, par, let, np.where(rng.random((N, 8, 1, S)) < 0.4, odd, txt))
def check_inputs(d):
    bad = []
    for k in ("let", "txt"):
        if np.min(d[k]) < 0 or np.max(d[k]) > 15: bad.append("range of " + k)
    par = np.stack([gentries(a) for a in d["par"]]).astype(np.int64); let = d["let"].astype(np.int64)
    for i in range(1, len(LEV)):
        m, o = LEV[i][1:]; part = par[:, :, o - LPR:o - LPR + m]
        if np.min(part) < 0 or np.max(part) >= LEV[i - 1][1]: bad.append("range of par on level " + str(i + 1))
    if bad: return bad
    want = np.zeros((N, 8, 16, C), np.int64)
    for i in range(1, len(LEV)):
        b, m, o = LEV[i]
        for r in range(N):
            want[r][A8, let[r, :, o - LPR:o - LPR + m], LEV[i - 1][2] + par[r, :, o - LPR:o - LPR + m]] = b + r * m + np.arange(m)
    if np.count_nonzero(want) != N * 8 * (C - LPR): bad.append("two states with one parent and letter")
    if not np.array_equal(want.reshape(N, 128, C), d["tri"]): bad.append("tri against par and let")
    return bad
def reference(tri, par, let, txt):
    t4 = tri.astype(np.int64).reshape(N, 8, 16, C); pl = np.stack([gentries(a) for a in par]).astype(np.int64)
    ll = let.astype(np.int64); tx = txt.astype(np.int64).reshape(N, 8, ST, S)
    G = np.zeros((8, 16, W), np.int64); G[:, :, 0] = 16 + np.arange(16)
    fail = np.zeros((8, W), np.int64)
    yg = np.zeros((N, 8, 16, C), np.int64); yf = np.zeros((N, 8, C), np.int64)
    for i in range(len(LEV)):
        b, m, o = LEV[i]
        for r in range(N):
            fl = np.zeros((8, m), np.int64)
            if i > 0:
                pb, pm = LEV[i - 1][:2]
                fp = np.take_along_axis(fail, pb + r * pm + pl[r, :, o - LPR:o - LPR + m], 1)
                fl = G[A8, ll[r, :, o - LPR:o - LPR + m], fp]
            own = t4[r, :, :, o:o + m]
            full = np.where(own != 0, own, np.take_along_axis(G, fl[:, None, :], 2))
            fail[:, b + r * m:b + (r + 1) * m] = fl; G[:, :, b + r * m:b + (r + 1) * m] = full
            yf[r, :, o:o + m] = fl; yg[r, :, :, o:o + m] = full
    s = np.zeros((N, 8, S), np.int64); big = np.zeros((N, 8, S), np.int64)
    for t in range(ST):
        s = G[np.arange(8)[None, :, None], tx[:, :, t], s]
        big = np.maximum(big, s)
    return {"yg": yg.reshape(N, 128, C).astype(np.float32), "yf": yf.astype(np.float32), "yl": s.astype(np.float32), "ym": big.astype(np.float32)}

@@ -1,0 +1,441 @@
+from concourse.bass import DstId, RemoteDMATransfer
+from concourse.mybir import AluOpType as A, ActivationFunctionType as F
+
+N = 8
+M = 384
+D = 0.0092
+K = 1.0 / D
+MID = 4752.0
+MAGIC = 12582912.0
+S1 = 40
+X2 = 32
+S2 = M + X2
+C3, C4, C5, CW = 256, 256 + N * M, 256 + 2 * N * M, 256 + 3 * N * M
+RELAY = {1: True, 2: True, 3: True, 4: False}
+
+
+def _bufs(where, dtype, **shapes):
+    return {k: (where, [128, v] if isinstance(v, int) else v, dtype) for k, v in shapes.items()}
+
+
+SCRATCH = {}
+SCRATCH.update(_bufs("sbuf", "int32", st1=N * S1, tb=2 * M, pr=74, tx=512, c01=64, lt=[8, 32], num=1184, pi=8, f4r=24))
+SCRATCH.update(_bufs("sbuf", "uint16", l5=N * 24, l23=N * 26, pru=74, pr3=24, txu=512, c01u=64, fl=16, lp=24, l34=24,
+                     lh=16, f4u=24, off=64, jl=32))
+SCRATCH.update(_bufs("sbuf", "bfloat16", st2=16 + N * S2, gt=CW, z=144, zc=144, idn=16, mk=1184, m2x=32, m3x=M, y3=M,
+                     yp=M, y4=M, e4=M, o4=M, hc=M, d4=M, h=256, t1e=16, xf=3 * M, tm=6 * 1024, xa=512, xb=512,
+                     xw=1024, ex=256, idr=256))
+SCRATCH.update(_bufs("sbuf", "float32", tbf=2 * M, yf0=[8, 34], pf=8, xio=144, cst=16, tmp=16, t1r=256, hp=256, f4=24,
+                     f4b=24, f5=24, yfl=72, ls=6 * 64, mx=64, ol=128, ygs=1186, c2=2))
+SCRATCH.update(_bufs("psum", "float32", pa=512, pb=512, pc=512, pd=512, pe=512, pg=512))
+SEMAPHORES = (["sv", "sa", "sp", "sg", "loc", "out", "i1", "ipar", "itb3", "itb4", "itx", "ilet"]
+              + ["p%d" % k for k in range(1, 5)] + ["d%dc%d" % (k, c) for k in range(1, 5) for c in range(N)])
+
+
+def rank_program(g, core, T, topo):
+    r = T.rank_of(core)
+    if r is None:
+        return
+    cores = list(T.cores)
+    chips = []
+    for c in cores:
+        if topo.chip(c) not in chips:
+            chips.append(topo.chip(c))
+    on = {ch: [c for c in cores if topo.chip(c) == ch] for ch in chips}
+    mine = topo.chip(core)
+    me = chips.index(mine)
+    place = on[mine].index(core)
+    mate = [c for c in on[mine] if c != core][0]
+    to_chips = [chips[(me + k) % len(chips)] for k in range(1, len(chips))]
+    from_chips = [chips[(me - k) % len(chips)] for k in range(1, len(chips))]
+    peers = [on[ch][place] for ch in to_chips]
+    far = peers + [c for ch in to_chips for c in on[ch] if c not in peers]
+    off_mask = topo.mask(core, far[0])
+    n_off = len(topo.engines(core, far[0]))
+    on_eng = [e for e in topo.engines(core, mate) if e not in topo.engines(core, far[0])]
+    on_mask = sum(1 << e for e in on_eng)
+    n_on = len(on_eng)
+    all_mask, n_all = topo.mask(core, mate), len(topo.engines(core, mate))
+
+    V, S, P, Y = g.vector, g.scalar, g.tensor, g.sync
+    queue = {"v": V, "a": S, "p": P, "g": g, "y": Y}
+    semof = {"v": "sv", "a": "sa", "p": "sp", "g": "sg"}
+    count = {"v": 0, "a": 0, "p": 0, "g": 0}
+    waited = {}
+    writer = {}
+    readers = {}
+    loc = [0]
+    outs = [0]
+
+    def wait(q, hs):
+        need = {}
+        for s, n in hs:
+            need[s] = max(need.get(s, 0), n)
+        for s, n in need.items():
+            if waited.get((q, s), 0) < n:
+                queue[q].wait_ge(T.sem[s], n)
+                waited[(q, s)] = n
+
+    def before(q, rd, wr):
+        hs = []
+        for k in rd:
+            hs += writer[k]
+        for k in wr:
+            hs += writer.get(k, []) + readers.get(k, [])
+        wait(q, hs)
+
+    def after(h, rd, wr):
+        for k in rd:
+            readers.setdefault(k, []).append(h)
+        for k in wr:
+            writer[k] = [h]
+            readers[k] = []
+
+    def op(q, fn, rd, wr):
+        before(q, rd, wr)
+        count[q] += 1
+        fn().then_inc(T.sem[semof[q]], 1)
+        after((semof[q], count[q]), rd, wr)
+
+    def load(q, out, in_, sem, key, total=16):
+        queue[q].dma_start(out, in_).then_inc(T.sem[sem], 16)
+        writer[key] = [(sem, total)]
+
+    def store(q, out, in_, rd):
+        before(q, rd, [])
+        queue[q].dma_start(out, in_).then_inc(T.sem.out, 16)
+        outs[0] += 16
+
+    def dst(c):
+        rid, pid, _se = topo.addr(c)
+        return DstId(rid=rid, pnc=pid)
+
+    def spread(rnd, ap, rd, split=False):
+        before("g", rd, [])
+        dests = peers if RELAY[rnd] else far
+        trs = [
+            RemoteDMATransfer(dst_ids=[dst(c) for c in dests], dma_engine_mask=off_mask,
+                              remote_sem=T.sem[("d%dc%d" % (rnd, me)) if RELAY[rnd] else "p%d" % rnd],
+                              srcs=[ap], dsts=[ap for c in dests]),
+            RemoteDMATransfer(dst_ids=[dst(mate)], dma_engine_mask=on_mask, remote_sem=T.sem["p%d" % rnd],
+                              srcs=[ap], dsts=[ap]),
+        ]
+        for part in ([trs[:1], trs[1:]] if split else [trs]):
+            g.remote_dma_fused(part, local_sem=T.sem.loc)
+        loc[0] += n_off + n_on
+
+    def wide(rnd):
+        return rnd == 2
+
+    def hand_on(rnd, ap_of):
+        if not RELAY[rnd]:
+            return
+        rid, pid, _se = topo.addr(mate)
+        for ch in from_chips:
+            wait("g", [("d%dc%d" % (rnd, chips.index(ch)), n_off)])
+            ap = ap_of(T.rank_of(on[ch][place]))
+            full = wide(rnd) and ch == from_chips[-1]
+            g.remote_dma(ap, ap, T.sem["p%d" % rnd], T.sem.loc, pid, rid, all_mask if full else on_mask)
+            loc[0] += n_all if full else n_on
+
+    def arrivals(rnd):
+        if not RELAY[rnd]:
+            return [("p%d" % rnd, n_off * len(far) + n_on)]
+        return ([("d%dc%d" % (rnd, chips.index(ch)), n_off) for ch in from_chips]
+                + [("p%d" % rnd, n_on * len(from_chips) + (n_all if wide(rnd) else n_on))])
+
+    def fold(ps, key, w, wkey, x, xkey):
+        before("p", [wkey, xkey], [key])
+        for i in range(16):
+            ins = P.matmul(ps, w[:, 15 - i:143 - i], x(i), i == 0, i == 15)
+        count["p"] += 1
+        ins.then_inc(T.sem.sp, 1)
+        after(("sp", count["p"]), [wkey, xkey], [key])
+
+    def ts(out, in0, s1, s2, o0, o1, rd, wr):
+        if o1 is None:
+            op("v", lambda: V.tensor_scalar(out, in0, s1, None, o0), rd, wr)
+        else:
+            op("v", lambda: V.tensor_scalar(out, in0, s1, s2, o0, o1), rd, wr)
+
+    def tt(out, in0, in1, o, rd, wr):
+        op("v", lambda: V.tensor_tensor(out, in0, in1, o), rd, wr)
+
+    def cp(out, in_, rd, wr):
+        op("v", lambda: V.tensor_copy(out, in_), rd, wr)
+
+    def act(out, in_, f, rd, wr, bias=0.0, scale=1.0):
+        op("a", lambda: S.activation(out, in_, f, bias=bias, scale=scale), rd, wr)
+
+    def enc(out, in_, rd, wr):
+        act(out, in_, F.Exp, rd, wr, bias=-D * MID, scale=D)
+
+    s1 = S1 * r
+    s2 = 16 + S2 * r
+    slot1 = lambda q: T.st1[:, S1 * q:S1 * (q + 1)]
+    slot2 = lambda q: T.st2[:, 16 + S2 * q:16 + S2 * (q + 1)]
+    slot4 = lambda q: T.gt[:, C4 + M * q:C4 + M * (q + 1)]
+    slot5 = lambda q: T.l5[:, 24 * q:24 * (q + 1)]
+    mk2, mk3, mk4, mk5 = T.mk[:, 0:32], T.mk[:, 32:416], T.mk[:, 416:800], T.mk[:, 800:1184]
+
+    load("y", slot1(r), T.tri[:, 0:S1], "i1", "own1")
+    load("y", T.pr[:], T.par[:], "ipar", "pr")
+    load("y", T.tb[:, 0:M], T.tri[:, 34:34 + M], "itb3", "tb3")
+    load("y", T.tb[:, M:2 * M], T.tri[:, 34 + M:34 + 2 * M], "itb4", "tb4")
+    for t in range(8):
+        load("y", T.tx[:, 64 * t:64 * t + 64], T.txt[:, 1024 * t:1024 * t + 1024], "itx", "tx", 128)
+    load("y", T.lt[:], T.let[:, 0:32], "ilet", "lt")
+
+    op("g", lambda: g.iota(T.pi[:, 0:1], [[1, 1]], 0, 1), [], ["pi0"])
+    op("g", lambda: g.iota(T.xio[:], [[1, 144]], -15, 0, allow_small_or_imprecise_dtypes=True), [], ["xio"])
+    op("g", lambda: g.iota(T.num[:, 0:32], [[1, 32]], 32 + 32 * r, 0), [], ["n2"])
+    op("g", lambda: g.iota(T.num[:, 32:416], [[1, M]], 288 + M * r, 0), [], ["n3"])
+    op("g", lambda: g.iota(T.cst[:], [[S1 - 32, 8], [0, 2]], -30, 0, allow_small_or_imprecise_dtypes=True), [], ["cst"])
+
+    spread(1, slot1(r), ["own1"], split=True)
+    writer["st1"] = writer["own1"] + arrivals(1)
+
+    for k, bits in enumerate([15, 112, 14, 1]):
+        ts(T.pi[:, 1 + k:2 + k], T.pi[:, 0:1], bits, None, A.bitwise_and, None, ["pi0"], ["pi%d" % (k + 1)])
+    cp(T.pf[:, 1:5], T.pi[:, 1:5], ["pi1", "pi2", "pi3", "pi4"], ["pf"])
+    pc, pgr = T.pf[:, 1:2], T.pf[:, 2:3]
+    ts(T.zc[:], T.xio[:], pgr, pc, A.is_equal, A.mult, ["xio", "pf"], ["zc"])
+    ts(T.z[:], T.xio[:], pgr, None, A.is_equal, None, ["xio", "pf"], ["z"])
+    ts(T.idn[:], T.xio[:, 15:31], pc, None, A.is_equal, None, ["xio", "pf"], ["idn"])
+    ts(T.pf[:, 5:6], T.pf[:, 3:4], S1 / 2.0, T.pf[:, 4:5], A.mult, A.add, ["pf"], ["pf5"])
+    op("v", lambda: V.memset(T.st2[:, 0:16], 0.0), [], ["null"])
+    op("v", lambda: V.memset(T.st2[:, s2 + M + 26:s2 + S2], 0.0), [], ["own2d"])
+    cp(T.jl[:, 0:16], T.xio[:, 15:31], ["xio"], ["jl0"])
+    ts(T.jl[:, 16:32], T.xio[:, 0:16], 0.0, pc, A.mult, A.add, ["xio", "pf"], ["jl1"])
+    ts(T.fl[:], T.xio[:, 0:16], 0.0, T.pf[:, 5:6], A.mult, A.add, ["xio", "pf5"], ["fl"])
+    op("v", lambda: V.memset(T.yf0[:, 0:2], 0.0), [], ["yf0a"])
+    act(T.idr[:], T.idn[:].indirect(T.jl[:, 16:32]), F.Copy, ["idn", "jl1"], ["idr"])
+
+    cp(T.pru[:], T.pr[:], ["pr"], ["pru"])
+    ts(T.pr3[:], T.pr[:, 2:26], 2.0, None, A.add, None, ["pr"], ["pr3"])
+    tt(mk2, T.st1[:, s1:s1 + 2].indirect(T.pru[:, 0:2]), T.num[:, 0:32], A.is_equal, ["own1", "pru", "n2"], ["mk2"])
+    fold(T.pg[:, 0:2], "pg", T.zc, "zc", lambda i: T.mk[:, i:32:16], "mk2")
+    ts(T.c2[:], T.pr[:, 0:2], 16.0, 32.0 * r, A.mult, A.add, ["pr"], ["c2"])
+    cp(T.tbf[:, 0:M], T.tb[:, 0:M], ["tb3"], ["tbf3"])
+    enc(T.st2[:, s2:s2 + M], T.tbf[:, 0:M], ["tbf3"], ["own2a"])
+    ts(T.m2x[:], mk2, 16.0, None, A.mult, None, ["mk2"], ["m2x"])
+    tt(mk3, T.st1[:, s1:s1 + 34].indirect(T.pr3[:]), T.num[:, 32:416], A.is_equal, ["own1", "pr3", "n3"], ["mk3"])
+    tt(T.y3[:], T.m2x[:].indirect(T.pru[:, 2:26]), mk3, A.add, ["m2x", "pru", "mk3"], ["y3"])
+    fold(T.pc[:, 0:24], "pc", T.zc, "zc", lambda i: T.y3[:, i::16], "y3")
+    tt(T.st2[:, s2 + M + 24:s2 + M + 26], T.c2[:], T.pg[:, 0:2], A.add, ["c2"], ["pg", "own2c"])
+    cp(T.tbf[:, M:2 * M], T.tb[:, M:2 * M], ["tb4"], ["tbf4"])
+    ts(T.num[:, 416:800], T.num[:, 32:416], float(N * M), None, A.add, None, ["n3"], ["n4"])
+    cp(T.st2[:, s2 + M:s2 + M + 24], T.pc[:, 0:24], [], ["pc", "own2b"])
+
+    own2 = ["own2a", "own2b", "own2c", "own2d"]
+    spread(2, slot2(r), own2)
+    hand_on(1, slot1)
+    hand_on(2, slot2)
+    writer["st2"] = sum([writer[k] for k in own2], writer["null"]) + arrivals(2)
+
+    enc(T.e4[:], T.tbf[:, M:2 * M], ["tbf4"], ["e4"])
+    act(T.yp[:], T.y3[:].indirect(T.pru[:, 26:50]), F.Copy, ["y3", "pru"], ["yp"])
+    fold(T.pd[:, 0:24], "pd", T.zc, "zc", lambda i: T.yp[:, i::16], "yp")
+
+    def tmk(t, a=0, b=64):
+        return T.tm[:, (t - 2) * 1024 + 16 * a:(t - 2) * 1024 + 16 * b]
+
+    def tmask(t, a=0, b=64):
+        act(tmk(t, a, b), T.idn[:].indirect(T.txu[:, 64 * t + a:64 * t + b]), F.Copy, ["idn", "txu"],
+            ["tm%d_%d" % (t, hh) for hh in range(2) if a <= 32 * hh < b])
+
+    def letters(q, rd):
+        cp(T.l23[:, 26 * q:26 * q + 26], T.st2[:, 16 + S2 * q + M:16 + S2 * q + M + 26], rd, ["l23_%d" % q])
+
+    l3of = lambda q: T.l23[:, 26 * q:26 * q + 24]
+    l2of = lambda q: T.l23[:, 26 * q + 24:26 * q + 26]
+
+    letters(r, ["own2b", "own2c"])
+    tt(mk4, T.tb[:, 0:M].indirect(T.pru[:, 26:50]), T.num[:, 416:800], A.is_equal, ["tb3", "pru", "n4"], ["mk4"])
+    cp(T.txu[:], T.tx[:], ["tx"], ["txu"])
+    tmask(2)
+    ts(T.m3x[:], mk3, 16.0, None, A.mult, None, ["mk3"], ["m3x"])
+    ts(T.c01[:], T.tx[:, 0:64], 16.0, None, A.mult, None, ["tx"], ["c01"])
+    tt(T.y4[:], T.m3x[:].indirect(T.pru[:, 26:50]), mk4, A.add, ["m3x", "pru", "mk4"], ["y4"])
+    fold(T.pe[:, 0:24], "pe", T.zc, "zc", lambda i: T.y4[:, i::16], "y4")
+    cp(T.lp[:], T.pd[:, 0:24], [], ["pd", "lp"])
+    tt(T.c01[:], T.c01[:], T.tx[:, 64:128], A.add, ["tx"], ["c01"])
+    ts(T.num[:, 800:1184], T.num[:, 32:416], float(2 * N * M), None, A.add, None, ["n3"], ["n5"])
+    cp(T.c01u[:], T.c01[:], ["c01"], ["c01u"])
+    tt(mk5, T.tb[:, M:2 * M].indirect(T.pru[:, 50:74]), T.num[:, 800:1184], A.is_equal, ["tb4", "pru", "n5"], ["mk5"])
+    tmask(3)
+    cp(T.l34[:], T.pe[:, 0:24], [], ["pe", "l34"])
+    cp(T.ygs[:, 0:2], T.st1[:, s1:s1 + 2], ["own1"], ["yg1"])
+    ts(T.yf0[:, 2:34], T.lt[:], 16.0, None, A.add, None, ["lt"], ["yf0b"])
+
+    tt(T.tmp[:], T.st1[:].indirect(T.fl[:, 0:1]), T.cst[:], A.add, ["st1", "fl", "cst"], ["tmp"])
+    cp(T.t1r[:], T.st1[:].indirect(T.fl[:]), ["st1", "fl"], ["t1r"])
+    cp(T.lh[:], T.tmp[:], ["tmp"], ["lh"])
+    tt(T.hp[:], T.st1[:].indirect(T.lh[:]), T.t1r[:], A.max, ["st1", "lh", "t1r"], ["hp"])
+    enc(T.t1e[:], T.t1r[:, 0:16], ["t1r"], ["t1e"])
+    enc(T.h[:], T.hp[:], ["hp"], ["h"])
+    act(T.ygs[:, 2:34], T.h[:].indirect(l2of(r)), F.Ln, ["h", "l23_%d" % r], ["yg2"])
+    tt(T.ex[:], T.t1e[:].indirect(T.jl[:, 0:16]), T.idr[:], A.mult, ["t1e", "jl0", "idr"], ["ex"])
+    x3, x4, x5 = T.xf[:, 0:M], T.xf[:, M:2 * M], T.xf[:, 2 * M:3 * M]
+    tt(x4, T.h[:].indirect(T.lp[:]), mk4, A.mult, ["h", "lp", "mk4"], ["x4"])
+    fold(T.pc[:, 0:24], "pc", T.z, "z", lambda i: T.xf[:, M + i:2 * M:16], "x4")
+
+    def level3(q):
+        tt(T.gt[:, C3 + M * q:C3 + M * (q + 1)], T.h[:].indirect(l3of(q)),
+           T.st2[:, 16 + S2 * q:16 + S2 * q + M], A.max,
+           ["h", "l23_%d" % q, "own2a" if q == r else "st2"], ["g3_%d" % q])
+
+    def decode_ln(a, n, src, rd, key):
+        act(T.ygs[:, a:a + n], src, F.Ln, rd, [key])
+
+    def decode_round(a, n, key):
+        act(T.ygs[:, a:a + n], T.ygs[:, a:a + n], F.Identity, [], [key], bias=MID + MAGIC, scale=K)
+
+    def decode_end(a, n, key):
+        act(T.ygs[:, a:a + n], T.ygs[:, a:a + n], F.Identity, [], [key], bias=-MAGIC)
+
+    tt(T.xw[:], T.h[:].indirect(T.c01u[:]), tmk(2), A.mult, ["h", "c01u", "tm2_0", "tm2_1"], ["xw"])
+    act(T.f4[:], T.pc[:, 0:24], F.Ln, [], ["pc", "f4"])
+    act(T.hc[:], T.h[:].indirect(T.l34[:]), F.Copy, ["h", "l34"], ["hc"])
+    fold(T.pe[:, 0:64], "pe", T.z, "z", lambda i: T.xw[:, i::16], "xw")
+    ts(T.f4r[:], T.f4[:], K / M, (MID - 288 - 191.5) / M, A.mult, A.add, ["f4"], ["f4r"])
+    ts(T.f4b[:], T.f4[:], K / X2, (MID - 288 + 16) / X2, A.mult, A.add, ["f4"], ["f4b"])
+    tt(T.f4b[:], T.f4b[:], T.f4r[:], A.add, ["f4r"], ["f4b"])
+    ts(T.f4u[:], T.f4b[:], float(X2), None, A.mult, None, ["f4b"], ["f4u"])
+    act(x3, T.ex[:].indirect(l3of(r)), F.Copy, ["ex", "l23_%d" % r], ["x3"])
+    act(T.ls[:, 64:128], T.pe[:, 0:64], F.Ln, [], ["pe", "ls2_0", "ls2_1"])
+    act(T.xw[:], T.ex[:].indirect(T.c01u[:]), F.Copy, ["ex", "c01u"], ["xw"])
+    fold(T.pe[:, 0:64], "pe", T.z, "z", lambda i: T.xw[:, i::16], "xw")
+    tt(T.o4[:], T.h[:].indirect(T.l34[:]), T.e4[:], A.max, ["h", "l34", "e4"], ["o4"])
+    level3(r)
+
+    tt(slot4(r), T.st2[:].indirect(T.f4u[:]), T.o4[:], A.max, ["st2", "f4u", "o4"], ["own4"])
+    spread(3, slot4(r), ["own4"])
+    tt(T.d4[:], T.st2[:].indirect(T.f4u[:]), T.hc[:], A.max, ["st2", "f4u", "hc"], ["d4"])
+    tt(x5, T.d4[:].indirect(T.pru[:, 50:74]), mk5, A.mult, ["d4", "pru", "mk5"], ["x5"])
+    fold(T.pd[:, 0:24], "pd", T.z, "z", lambda i: T.xf[:, 2 * M + i:3 * M:16], "x5")
+    decode_ln(34, M, T.gt[:, C3 + M * r:C3 + M * (r + 1)], ["g3_%d" % r], "yg3")
+    act(T.ls[:, 0:64], T.pe[:, 0:64], F.Ln, [], ["pe", "ls1_0", "ls1_1"])
+    decode_ln(34 + M, M, slot4(r), ["own4"], "yg4")
+    act(T.f5[:], T.pd[:, 0:24], F.Ln, [], ["pd", "f5"])
+    rest = [q for q in range(N) if q != r]
+    for q in rest:
+        letters(q, ["st2"])
+    level3(rest[0])
+    level3(rest[1])
+    ts(slot5(r), T.f5[:], K, MID - 32, A.mult, A.add, ["f5"], ["own5"])
+    spread(4, slot5(r), ["own5"])
+    hand_on(3, slot4)
+    hand_on(4, slot5)
+    writer["l5"] = writer["own5"] + arrivals(4)
+    writer["g4"] = writer["own4"] + arrivals(3)
+
+    for q in range(N):
+        act(T.gt[:, 32 * q:32 * q + 32], T.h[:].indirect(l2of(q)), F.Copy, ["h", "l23_%d" % q], ["g2_%d" % q])
+    tmask(4)
+    tmask(5)
+    ts(T.off[:], T.ls[:, 64:128], K, MID - 32, A.mult, A.add, ["ls2_0", "ls2_1"], ["off0", "off1"])
+    for q in rest[2:]:
+        level3(q)
+    for d in range(3):
+        fold(T.pg[:, 24 * d:24 * d + 24], "pg", T.z, "z",
+             lambda i: T.xf[:, M * d + 24 * i:M * d + 24 * (i + 1)], "x%d" % (d + 3))
+    act(T.yfl[:], T.pg[:, 0:72], F.Ln, [], ["pg", "yfl"])
+    writer["yg24"] = writer["yg2"] + writer["yg3"] + writer["yg4"]
+
+    xs, ps = [T.xa, T.xb], [T.pa, T.pb]
+    g3keys = ["g2_%d" % q for q in range(N)] + ["g3_%d" % q for q in range(N)]
+    g5keys = ["g5_%d" % k for k in range(6)]
+
+    def lsout(t, hh):
+        return T.ol[:, 32 * hh:32 * hh + 32] if t == 7 else T.ls[:, 64 * (t - 1) + 32 * hh:64 * (t - 1) + 32 * hh + 32]
+
+    def look(t, hh):
+        top, keys = (C4, g3keys) if t == 3 else (C5, g3keys + ["g4"]) if t == 4 else (CW, g3keys + ["g4"] + g5keys)
+        tt(xs[hh][:], T.gt[:, 0:top].indirect(T.off[:, 32 * hh:32 * hh + 32]), tmk(t, 32 * hh, 32 * hh + 32), A.mult,
+           keys + ["off%d" % hh, "tm%d_%d" % (t, hh)], ["x_%d" % hh])
+        fold(ps[hh][:, 0:32], "ps%d" % hh, T.z, "z", lambda i: xs[hh][:, i::16], "x_%d" % hh)
+
+    def ln(t, hh):
+        act(lsout(t, hh), ps[hh][:, 0:32], F.Ln, [], ["ps%d" % hh, "ls%d_%d" % (t, hh)])
+
+    def nxt(t, hh):
+        ts(T.off[:, 32 * hh:32 * hh + 32], lsout(t, hh), K, MID - 32, A.mult, A.add,
+           ["ls%d_%d" % (t, hh)], ["off%d" % hh])
+
+    def most(t):
+        tt(T.mx[:], T.mx[:], T.ls[:, 64 * (t - 1):64 * t], A.max, ["ls%d_0" % t, "ls%d_1" % t], ["mx"])
+
+    look(3, 0)
+    look(3, 1)
+    ts(T.ygs[:, 2:802], T.ygs[:, 2:802], K, MID + MAGIC, A.mult, A.add, [], ["yg24"])
+    ln(3, 0)
+    decode_end(2, 800, "yg24")
+    ln(3, 1)
+    ts(T.yfl[:], T.yfl[:], K, MID + MAGIC, A.mult, A.add, [], ["yfl"])
+    tt(T.mx[:], T.ls[:, 0:64], T.ls[:, 64:128], A.max, ["ls1_0", "ls1_1", "ls2_0", "ls2_1"], ["mx"])
+    ts(T.yfl[:], T.yfl[:], -MAGIC, None, A.add, None, [], ["yfl"])
+    nxt(3, 0)
+
+    def level5(q, k):
+        out = T.gt[:, C5 + 512 * k:C5 + 512 * (k + 1)]
+        src = T.gt[:, 0:C5].indirect(T.l5[:, 32 * k:32 * k + 32])
+        rd = g3keys + ["g4", "l5"]
+        if q == "a":
+            act(out, src, F.Copy, rd, ["g5_%d" % k])
+        else:
+            cp(out, src, rd, ["g5_%d" % k])
+
+    look(4, 0)
+    store("y", T.yg[:, 0:802], T.ygs[:, 0:802], ["yg1", "yg24", "g4"])
+    store("y", T.yf[:, 0:34], T.yf0[:], ["yf0a", "yf0b"])
+    for d in range(3):
+        store("y", T.yf[:, 34 + M * d:34 + M * (d + 1)], T.yfl[:, 24 * d:24 * d + 24], ["yfl"])
+    level5("a", 0)
+    nxt(3, 1)
+    look(4, 1)
+    most(3)
+    level5("a", 1)
+    level5("a", 2)
+    level5("v", 4)
+    ln(4, 0)
+    level5("v", 5)
+    level5("a", 3)
+    ln(4, 1)
+    nxt(4, 0)
+    look(5, 0)
+    nxt(4, 1)
+    tmask(6, 0, 32)
+    decode_ln(802, M, T.gt[:, C5 + M * r:C5 + M * (r + 1)], g5keys, "yg5")
+    look(5, 1)
+    decode_round(802, M, "yg5")
+    most(4)
+    ln(5, 0)
+    tmask(6, 32, 64)
+    nxt(5, 0)
+    look(6, 0)
+    ln(5, 1)
+    tmask(7, 0, 32)
+    nxt(5, 1)
+    look(6, 1)
+    most(5)
+    ln(6, 0)
+    tmask(7, 32, 64)
+    nxt(6, 0)
+    look(7, 0)
+    ln(6, 1)
+    decode_end(802, M, "yg5")
+    store("y", T.yg[:, 802:1186], T.ygs[:, 802:1186], ["yg5"])
+    nxt(6, 1)
+    look(7, 1)
+    most(6)
+    ln(7, 0)
+    ln(7, 1)
+    tt(T.ol[:, 64:128], T.mx[:], T.ol[:, 0:64], A.max, ["mx", "ls7_0", "ls7_1"], ["ol"])
+    ts(T.ol[:], T.ol[:], K, MID + MAGIC, A.mult, A.add, [], ["ol"])
+    ts(T.ol[:], T.ol[:], -MAGIC, None, A.add, None, [], ["ol"])
+    store("y", T.yl[:], T.ol[:, 0:64], ["ol"])
+    store("a", T.ym[:], T.ol[:, 64:128], ["ol"])
+
+    wait("g", [("loc", loc[0])])
+    wait("y", [("sv", count["v"]), ("sa", count["a"]), ("sp", count["p"]), ("sg", count["g"]), ("out", outs[0])])

@@ -7,11 +7,20 @@ D = 0.0092
 K = 1.0 / D
 MID = 4752.0
 MAGIC = 12582912.0
-S1 = 40
-X2 = 32
-S2 = M + X2
+S1 = 64
+S3 = M + 32
 C3, C4, C5, CW = 256, 256 + N * M, 256 + 2 * N * M, 256 + 3 * N * M
-RELAY = {1: True, 2: True, 3: True, 4: False}
+ORDER = """
+t12:a pi0 nfa xio ltz:v pf tb4:y tx0:y tx5:y pr:a lt:y tb3:y tx7:y tx3:y tx6:y tx2:y tx4:y tx1:y nea lo1 lab idn own1
+nfb z jl1 idr neb w3a yf0 pru zc y3 fy3 tbf3 tbf4 l3own yp enc4 enc3 fyp txu3 txu5 blk lc_0 words w3b mk4 send1 tm3a:a
+yg1 send1m send4h send3 lp ex txu6 t1r h txu4 n2r x4 lc_1 lev3_1 fx4 n5 x3 n2c tm5a:a n2l f4 w3 w3n l4own lev3_0 lc_2
+lev3_2 lc_3 z01 lev3_3 mk5 tm4b:a xp fxp s2:a tm3b:a fp sl4 sx3_1:n sx3_2:w sx3_3:w tm6a:a fs2 g2 f4p d4_3 ls2
+sx4_3:fw txu7 x5 lev4_2 fx5 f5 off3 own5 lev4_0 lev4_1 tm4a:a yg2 fyf3 fs1 ls1 yg4 tm7b:a yg3 rnB:a tm7a:a fyf4
+look3a:F ln3a rnA:a sl5 sx4_2:n sx4_1:w lev4_3 tm5b:v nxt4a mx look4a:F fyf5 l5_2:a l5_0:a l5_1:a l5_3:a ln4a l5_7:a
+l5_5:v l5_6:v l5_4:v nxt5a look5a yg5 sbB:a sbA:a ln5a tm6b:a look5b nxt6a look6a ln5b ln6a nxt6b most5 look6b nxt7a
+most4 look7a ln6b rnC:a sbC:a ln7a yfl:a nxt7b look7b ln7b most6 enda endb d4_1 d4_2 look3b ln3b nxt4b sx3_0:j d4_0
+sx4_0:j ln4b nxt5b look4b
+""".split()
 
 
 def _bufs(where, dtype, **shapes):
@@ -19,23 +28,22 @@ def _bufs(where, dtype, **shapes):
 
 
 SCRATCH = {}
-SCRATCH.update(_bufs("sbuf", "int32", st1=N * S1, tb=2 * M, pr=74, tx=512, c01=64, lt=[8, 32], num=1184, pi=8, f4r=24))
-SCRATCH.update(_bufs("sbuf", "uint16", l5=N * 24, l23=N * 26, pru=74, pr3=24, txu=512, c01u=64, fl=16, lp=24, l34=24,
-                     lh=16, f4u=24, off=64, jl=32))
-SCRATCH.update(_bufs("sbuf", "bfloat16", st2=16 + N * S2, gt=CW, z=144, zc=144, idn=16, mk=1184, m2x=32, m3x=M, y3=M,
-                     yp=M, y4=M, e4=M, o4=M, hc=M, d4=M, h=256, t1e=16, xf=3 * M, tm=6 * 1024, xa=512, xb=512,
-                     xw=1024, ex=256, idr=256))
-SCRATCH.update(_bufs("sbuf", "float32", tbf=2 * M, yf0=[8, 34], pf=8, xio=144, cst=16, tmp=16, t1r=256, hp=256, f4=24,
-                     f4b=24, f5=24, yfl=72, ls=6 * 64, mx=64, ol=128, ygs=1186, c2=2))
-SCRATCH.update(_bufs("psum", "float32", pa=512, pb=512, pc=512, pd=512, pe=512, pg=512))
-SEMAPHORES = (["sv", "sa", "sp", "sg", "loc", "out", "i1", "ipar", "itb3", "itb4", "itx", "ilet"]
-              + ["p%d" % k for k in range(1, 5)] + ["d%dc%d" % (k, c) for k in range(1, 5) for c in range(N)])
+SCRATCH.update(_bufs("sbuf", "int32", t12=40, tb=2 * M, pr=74, tx=512, lt=416, l16=32, pi=8, n5=M))
+SCRATCH.update(_bufs("sbuf", "uint16", l3=4 * 24, l4=4 * 24, l5=N * 24, pru=74, txu=512, w2u=64,
+                     lo=4, l2=16, la=16, lb=16, lp=24, f4p=24, off=5 * 64, jl=32))
+SCRATCH.update(_bufs("sbuf", "bfloat16", st1=N * S1, rw3=4 * S3, rw4=4 * M, d4=4 * M, gt=CW, z=144, z0=144, z1=144,
+                     idn=16, blk=128, mk=2 * M, y3=M, yp=M, xp=M, h=256, t1r=256, xf=3 * M, tm=5 * 1024,
+                     xs=5 * 1024, xw=1024, ex=256, n2r=256, idr=256, ne=M, w3=4096))
+SCRATCH.update(_bufs("sbuf", "float32", tbf=2 * M, nf=M, f48=S1, yf0=34, pf=12, xio=144, n2=16, f4=24,
+                     fp=24, f5=24, yfl=72, ls=6 * 64, mx=64, ol=128, oo=128, ygs=1186, c01=64, w2=64, bio=128))
+SCRATCH.update(_bufs("psum", "float32", pa=512, pb=512, pc=512, pd=512, pe=512, pg=512, ph=512))
+SEMAPHORES = (["sv", "sa", "sp", "sg", "loc", "out", "iw", "hs", "h5", "r1", "x3", "x4", "r5", "q5", "al4",
+               "it12", "ilt", "itb3", "itb4", "ipr"] + ["itx%d" % t for t in range(8)]
+              + ["%s%d" % (k, c) for k in ("a3", "a4") for c in range(4)])
+OPT = {}
 
 
 def rank_program(g, core, T, topo):
-    r = T.rank_of(core)
-    if r is None:
-        return
     cores = list(T.cores)
     chips = []
     for c in cores:
@@ -43,19 +51,44 @@ def rank_program(g, core, T, topo):
             chips.append(topo.chip(c))
     on = {ch: [c for c in cores if topo.chip(c) == ch] for ch in chips}
     mine = topo.chip(core)
+    if mine not in chips:
+        return
     me = chips.index(mine)
-    place = on[mine].index(core)
-    mate = [c for c in on[mine] if c != core][0]
     to_chips = [chips[(me + k) % len(chips)] for k in range(1, len(chips))]
     from_chips = [chips[(me - k) % len(chips)] for k in range(1, len(chips))]
+    helpers = [c for c in topo.cores_of(core) if topo.die(c) != topo.die(on[mine][0])
+               and all(topo.may_write(c, d) for ch in to_chips for d in on[ch])]
+
+    def dst(c):
+        rid, pid, _se = topo.addr(c)
+        return DstId(rid=rid, pnc=pid)
+
+    r = T.rank_of(core)
+    place = on[mine].index(core) if r is not None else helpers.index(core) if core in helpers[:2] else None
+    if place is None:
+        return
     peers = [on[ch][place] for ch in to_chips]
-    far = peers + [c for ch in to_chips for c in on[ch] if c not in peers]
-    off_mask = topo.mask(core, far[0])
-    n_off = len(topo.engines(core, far[0]))
-    on_eng = [e for e in topo.engines(core, mate) if e not in topo.engines(core, far[0])]
-    on_mask = sum(1 << e for e in on_eng)
+    others = [c for ch in to_chips for c in on[ch] if c not in peers]
+    off_mask = topo.mask(core, peers[0])
+    n_off = len(topo.engines(core, peers[0]))
+    mate = [c for c in on[mine] if c != core][0]
+    all_eng = topo.engines(core, mate)
+    on_eng = [e for e in all_eng if e not in topo.engines(core, peers[0])]
+    bits = lambda es: sum(1 << e for e in es)
     n_on = len(on_eng)
-    all_mask, n_all = topo.mask(core, mate), len(topo.engines(core, mate))
+    if r is None:
+        q = 2 * me + place
+        for sem, n_in, ap, to, there in (("hs", n_on, T.rw4[:, M * me:M * (me + 1)], peers, "a4%d" % me),
+                                         ("h5", n_on // 2, T.l5[:, 24 * q:24 * q + 24], others, "q5")):
+            g.wait_ge(T.sem[sem], n_in)
+            g.remote_dma_fused([RemoteDMATransfer(dst_ids=[dst(c) for c in to], dma_engine_mask=off_mask,
+                                                  remote_sem=T.sem[there], srcs=[ap], dsts=[ap for c in to])],
+                               local_sem=T.sem.loc)
+        g.wait_ge(T.sem.loc, 2 * n_off)
+        return
+    assert r == 2 * me + place
+    order = [me] + [chips.index(ch) for ch in from_chips]
+    rank_of = lambda j: 2 * order[j] + place
 
     V, S, P, Y = g.vector, g.scalar, g.tensor, g.sync
     queue = {"v": V, "a": S, "p": P, "g": g, "y": Y}
@@ -66,6 +99,7 @@ def rank_program(g, core, T, topo):
     readers = {}
     loc = [0]
     outs = [0]
+    var = dict(x.partition(":")[::2] for x in ORDER)
 
     def wait(q, hs):
         need = {}
@@ -97,60 +131,52 @@ def rank_program(g, core, T, topo):
         fn().then_inc(T.sem[semof[q]], 1)
         after((semof[q], count[q]), rd, wr)
 
-    def load(q, out, in_, sem, key, total=16):
-        queue[q].dma_start(out, in_).then_inc(T.sem[sem], 16)
-        writer[key] = [(sem, total)]
+    def load(key, out, in_, rd=()):
+        before(var[key], rd, [])
+        queue[var[key]].dma_start(out, in_).then_inc(T.sem["i" + key], 16)
+        writer[key] = [("i" + key, 16)]
 
     def store(q, out, in_, rd):
         before(q, rd, [])
         queue[q].dma_start(out, in_).then_inc(T.sem.out, 16)
         outs[0] += 16
 
-    def dst(c):
-        rid, pid, _se = topo.addr(c)
-        return DstId(rid=rid, pnc=pid)
-
-    def spread(rnd, ap, rd, split=False):
+    def send(ap, rd, *parts):
         before("g", rd, [])
-        dests = peers if RELAY[rnd] else far
-        trs = [
-            RemoteDMATransfer(dst_ids=[dst(c) for c in dests], dma_engine_mask=off_mask,
-                              remote_sem=T.sem[("d%dc%d" % (rnd, me)) if RELAY[rnd] else "p%d" % rnd],
-                              srcs=[ap], dsts=[ap for c in dests]),
-            RemoteDMATransfer(dst_ids=[dst(mate)], dma_engine_mask=on_mask, remote_sem=T.sem["p%d" % rnd],
-                              srcs=[ap], dsts=[ap]),
-        ]
-        for part in ([trs[:1], trs[1:]] if split else [trs]):
-            g.remote_dma_fused(part, local_sem=T.sem.loc)
-        loc[0] += n_off + n_on
+        g.remote_dma_fused([RemoteDMATransfer(dst_ids=[dst(c) for c in cs], dma_engine_mask=m, remote_sem=T.sem[s],
+                                              srcs=[ap], dsts=[ap for c in cs]) for cs, m, n, s in parts],
+                           local_sem=T.sem.loc)
+        loc[0] += sum(n for cs, m, n, s in parts)
 
-    def wide(rnd):
-        return rnd == 2
+    off = lambda cs, s: (cs, off_mask, n_off, s)
+    near = lambda c, s, es=on_eng: ([c], bits(es), len(es), s)
 
-    def hand_on(rnd, ap_of):
-        if not RELAY[rnd]:
-            return
-        rid, pid, _se = topo.addr(mate)
-        for ch in from_chips:
-            wait("g", [("d%dc%d" % (rnd, chips.index(ch)), n_off)])
-            ap = ap_of(T.rank_of(on[ch][place]))
-            full = wide(rnd) and ch == from_chips[-1]
-            g.remote_dma(ap, ap, T.sem["p%d" % rnd], T.sem.loc, pid, rid, all_mask if full else on_mask)
-            loc[0] += n_all if full else n_on
+    def calls(d):
+        out, cur = {}, []
+        for j in range(4):
+            cur.append(j)
+            if "j" not in var["sx%d_%d" % (d, j)] or j == 3:
+                es = all_eng if "w" in var["sx%d_%d" % (d, j)] else on_eng
+                n = len(es) // (4 if len(cur) > 2 else len(cur))
+                out[j] = [(x, bits(es[n * i:n * i + n]), n) for i, x in enumerate(cur)]
+                cur = []
+        return out
 
-    def arrivals(rnd):
-        if not RELAY[rnd]:
-            return [("p%d" % rnd, n_off * len(far) + n_on)]
-        return ([("d%dc%d" % (rnd, chips.index(ch)), n_off) for ch in from_chips]
-                + [("p%d" % rnd, n_on * len(from_chips) + (n_all if wide(rnd) else n_on))])
+    def pieces(d, j, part):
+        if j in calls(d):
+            before("g", sum([part(x)[1] for x, m, n in calls(d)[j]], []), [])
+            g.remote_dma_fused([RemoteDMATransfer(dst_ids=[dst(mate)], dma_engine_mask=m, remote_sem=T.sem["x%d" % d],
+                                                  srcs=part(x)[2], dsts=[part(x)[0]], alu_op=2 * (len(part(x)[2]) - 1))
+                                for x, m, n in calls(d)[j]], local_sem=T.sem.loc)
+            loc[0] += sum(n for x, m, n in calls(d)[j])
 
-    def fold(ps, key, w, wkey, x, xkey):
-        before("p", [wkey, xkey], [key])
+    def fold(bank, a, n, w, x, xkeys, key):
+        before("p", [w] + xkeys, [bank])
         for i in range(16):
-            ins = P.matmul(ps, w[:, 15 - i:143 - i], x(i), i == 0, i == 15)
+            ins = P.matmul(T[bank][:, a:a + n], T[w][:, 15 - i:143 - i], x(i), i == 0, i == 15)
         count["p"] += 1
         ins.then_inc(T.sem.sp, 1)
-        after(("sp", count["p"]), [wkey, xkey], [key])
+        after(("sp", count["p"]), [w] + xkeys, [bank, key])
 
     def ts(out, in0, s1, s2, o0, o1, rd, wr):
         if o1 is None:
@@ -167,275 +193,324 @@ def rank_program(g, core, T, topo):
     def act(out, in_, f, rd, wr, bias=0.0, scale=1.0):
         op("a", lambda: S.activation(out, in_, f, bias=bias, scale=scale), rd, wr)
 
+    def copy(name, out, in_, rd, wr):
+        if var[name] == "v":
+            cp(out, in_, rd, wr)
+        else:
+            act(out, in_, F.Copy, rd, wr)
+
     def enc(out, in_, rd, wr):
         act(out, in_, F.Exp, rd, wr, bias=-D * MID, scale=D)
 
-    s1 = S1 * r
-    s2 = 16 + S2 * r
-    slot1 = lambda q: T.st1[:, S1 * q:S1 * (q + 1)]
-    slot2 = lambda q: T.st2[:, 16 + S2 * q:16 + S2 * (q + 1)]
-    slot4 = lambda q: T.gt[:, C4 + M * q:C4 + M * (q + 1)]
-    slot5 = lambda q: T.l5[:, 24 * q:24 * (q + 1)]
-    mk2, mk3, mk4, mk5 = T.mk[:, 0:32], T.mk[:, 32:416], T.mk[:, 416:800], T.mk[:, 800:1184]
+    def tolist(out, in_, rd, wr):
+        ts(out, in_, K, MID - 32, A.mult, A.add, rd, wr)
 
-    load("y", slot1(r), T.tri[:, 0:S1], "i1", "own1")
-    load("y", T.pr[:], T.par[:], "ipar", "pr")
-    load("y", T.tb[:, 0:M], T.tri[:, 34:34 + M], "itb3", "tb3")
-    load("y", T.tb[:, M:2 * M], T.tri[:, 34 + M:34 + 2 * M], "itb4", "tb4")
-    for t in range(8):
-        load("y", T.tx[:, 64 * t:64 * t + 64], T.txt[:, 1024 * t:1024 * t + 1024], "itx", "tx", 128)
-    load("y", T.lt[:], T.let[:, 0:32], "ilet", "lt")
+    def fill(ap, key, value=0.0):
+        op("v", lambda: V.memset(ap, value), [], [key])
 
-    op("g", lambda: g.iota(T.pi[:, 0:1], [[1, 1]], 0, 1), [], ["pi0"])
-    op("g", lambda: g.iota(T.xio[:], [[1, 144]], -15, 0, allow_small_or_imprecise_dtypes=True), [], ["xio"])
-    op("g", lambda: g.iota(T.num[:, 0:32], [[1, 32]], 32 + 32 * r, 0), [], ["n2"])
-    op("g", lambda: g.iota(T.num[:, 32:416], [[1, M]], 288 + M * r, 0), [], ["n3"])
-    op("g", lambda: g.iota(T.cst[:], [[S1 - 32, 8], [0, 2]], -30, 0, allow_small_or_imprecise_dtypes=True), [], ["cst"])
+    def iota(out, pattern, base, mult, key, **kw):
+        op("g", lambda: g.iota(out, pattern, base, mult, **kw), [], [key])
 
-    spread(1, slot1(r), ["own1"], split=True)
-    writer["st1"] = writer["own1"] + arrivals(1)
-
-    for k, bits in enumerate([15, 112, 14, 1]):
-        ts(T.pi[:, 1 + k:2 + k], T.pi[:, 0:1], bits, None, A.bitwise_and, None, ["pi0"], ["pi%d" % (k + 1)])
-    cp(T.pf[:, 1:5], T.pi[:, 1:5], ["pi1", "pi2", "pi3", "pi4"], ["pf"])
-    pc, pgr = T.pf[:, 1:2], T.pf[:, 2:3]
-    ts(T.zc[:], T.xio[:], pgr, pc, A.is_equal, A.mult, ["xio", "pf"], ["zc"])
-    ts(T.z[:], T.xio[:], pgr, None, A.is_equal, None, ["xio", "pf"], ["z"])
-    ts(T.idn[:], T.xio[:, 15:31], pc, None, A.is_equal, None, ["xio", "pf"], ["idn"])
-    ts(T.pf[:, 5:6], T.pf[:, 3:4], S1 / 2.0, T.pf[:, 4:5], A.mult, A.add, ["pf"], ["pf5"])
-    op("v", lambda: V.memset(T.st2[:, 0:16], 0.0), [], ["null"])
-    op("v", lambda: V.memset(T.st2[:, s2 + M + 26:s2 + S2], 0.0), [], ["own2d"])
-    cp(T.jl[:, 0:16], T.xio[:, 15:31], ["xio"], ["jl0"])
-    ts(T.jl[:, 16:32], T.xio[:, 0:16], 0.0, pc, A.mult, A.add, ["xio", "pf"], ["jl1"])
-    ts(T.fl[:], T.xio[:, 0:16], 0.0, T.pf[:, 5:6], A.mult, A.add, ["xio", "pf5"], ["fl"])
-    op("v", lambda: V.memset(T.yf0[:, 0:2], 0.0), [], ["yf0a"])
-    act(T.idr[:], T.idn[:].indirect(T.jl[:, 16:32]), F.Copy, ["idn", "jl1"], ["idr"])
-
-    cp(T.pru[:], T.pr[:], ["pr"], ["pru"])
-    ts(T.pr3[:], T.pr[:, 2:26], 2.0, None, A.add, None, ["pr"], ["pr3"])
-    tt(mk2, T.st1[:, s1:s1 + 2].indirect(T.pru[:, 0:2]), T.num[:, 0:32], A.is_equal, ["own1", "pru", "n2"], ["mk2"])
-    fold(T.pg[:, 0:2], "pg", T.zc, "zc", lambda i: T.mk[:, i:32:16], "mk2")
-    ts(T.c2[:], T.pr[:, 0:2], 16.0, 32.0 * r, A.mult, A.add, ["pr"], ["c2"])
-    cp(T.tbf[:, 0:M], T.tb[:, 0:M], ["tb3"], ["tbf3"])
-    enc(T.st2[:, s2:s2 + M], T.tbf[:, 0:M], ["tbf3"], ["own2a"])
-    ts(T.m2x[:], mk2, 16.0, None, A.mult, None, ["mk2"], ["m2x"])
-    tt(mk3, T.st1[:, s1:s1 + 34].indirect(T.pr3[:]), T.num[:, 32:416], A.is_equal, ["own1", "pr3", "n3"], ["mk3"])
-    tt(T.y3[:], T.m2x[:].indirect(T.pru[:, 2:26]), mk3, A.add, ["m2x", "pru", "mk3"], ["y3"])
-    fold(T.pc[:, 0:24], "pc", T.zc, "zc", lambda i: T.y3[:, i::16], "y3")
-    tt(T.st2[:, s2 + M + 24:s2 + M + 26], T.c2[:], T.pg[:, 0:2], A.add, ["c2"], ["pg", "own2c"])
-    cp(T.tbf[:, M:2 * M], T.tb[:, M:2 * M], ["tb4"], ["tbf4"])
-    ts(T.num[:, 416:800], T.num[:, 32:416], float(N * M), None, A.add, None, ["n3"], ["n4"])
-    cp(T.st2[:, s2 + M:s2 + M + 24], T.pc[:, 0:24], [], ["pc", "own2b"])
-
-    own2 = ["own2a", "own2b", "own2c", "own2d"]
-    spread(2, slot2(r), own2)
-    hand_on(1, slot1)
-    hand_on(2, slot2)
-    writer["st2"] = sum([writer[k] for k in own2], writer["null"]) + arrivals(2)
-
-    enc(T.e4[:], T.tbf[:, M:2 * M], ["tbf4"], ["e4"])
-    act(T.yp[:], T.y3[:].indirect(T.pru[:, 26:50]), F.Copy, ["y3", "pru"], ["yp"])
-    fold(T.pd[:, 0:24], "pd", T.zc, "zc", lambda i: T.yp[:, i::16], "yp")
-
-    def tmk(t, a=0, b=64):
-        return T.tm[:, (t - 2) * 1024 + 16 * a:(t - 2) * 1024 + 16 * b]
-
-    def tmask(t, a=0, b=64):
-        act(tmk(t, a, b), T.idn[:].indirect(T.txu[:, 64 * t + a:64 * t + b]), F.Copy, ["idn", "txu"],
-            ["tm%d_%d" % (t, hh) for hh in range(2) if a <= 32 * hh < b])
-
-    def letters(q, rd):
-        cp(T.l23[:, 26 * q:26 * q + 26], T.st2[:, 16 + S2 * q + M:16 + S2 * q + M + 26], rd, ["l23_%d" % q])
-
-    l3of = lambda q: T.l23[:, 26 * q:26 * q + 24]
-    l2of = lambda q: T.l23[:, 26 * q + 24:26 * q + 26]
-
-    letters(r, ["own2b", "own2c"])
-    tt(mk4, T.tb[:, 0:M].indirect(T.pru[:, 26:50]), T.num[:, 416:800], A.is_equal, ["tb3", "pru", "n4"], ["mk4"])
-    cp(T.txu[:], T.tx[:], ["tx"], ["txu"])
-    tmask(2)
-    ts(T.m3x[:], mk3, 16.0, None, A.mult, None, ["mk3"], ["m3x"])
-    ts(T.c01[:], T.tx[:, 0:64], 16.0, None, A.mult, None, ["tx"], ["c01"])
-    tt(T.y4[:], T.m3x[:].indirect(T.pru[:, 26:50]), mk4, A.add, ["m3x", "pru", "mk4"], ["y4"])
-    fold(T.pe[:, 0:24], "pe", T.zc, "zc", lambda i: T.y4[:, i::16], "y4")
-    cp(T.lp[:], T.pd[:, 0:24], [], ["pd", "lp"])
-    tt(T.c01[:], T.c01[:], T.tx[:, 64:128], A.add, ["tx"], ["c01"])
-    ts(T.num[:, 800:1184], T.num[:, 32:416], float(2 * N * M), None, A.add, None, ["n3"], ["n5"])
-    cp(T.c01u[:], T.c01[:], ["c01"], ["c01u"])
-    tt(mk5, T.tb[:, M:2 * M].indirect(T.pru[:, 50:74]), T.num[:, 800:1184], A.is_equal, ["tb4", "pru", "n5"], ["mk5"])
-    tmask(3)
-    cp(T.l34[:], T.pe[:, 0:24], [], ["pe", "l34"])
-    cp(T.ygs[:, 0:2], T.st1[:, s1:s1 + 2], ["own1"], ["yg1"])
-    ts(T.yf0[:, 2:34], T.lt[:], 16.0, None, A.add, None, ["lt"], ["yf0b"])
-
-    tt(T.tmp[:], T.st1[:].indirect(T.fl[:, 0:1]), T.cst[:], A.add, ["st1", "fl", "cst"], ["tmp"])
-    cp(T.t1r[:], T.st1[:].indirect(T.fl[:]), ["st1", "fl"], ["t1r"])
-    cp(T.lh[:], T.tmp[:], ["tmp"], ["lh"])
-    tt(T.hp[:], T.st1[:].indirect(T.lh[:]), T.t1r[:], A.max, ["st1", "lh", "t1r"], ["hp"])
-    enc(T.t1e[:], T.t1r[:, 0:16], ["t1r"], ["t1e"])
-    enc(T.h[:], T.hp[:], ["hp"], ["h"])
-    act(T.ygs[:, 2:34], T.h[:].indirect(l2of(r)), F.Ln, ["h", "l23_%d" % r], ["yg2"])
-    tt(T.ex[:], T.t1e[:].indirect(T.jl[:, 0:16]), T.idr[:], A.mult, ["t1e", "jl0", "idr"], ["ex"])
+    slot1 = T.st1[:, S1 * r:S1 * (r + 1)]
+    raw3 = lambda j: T.rw3[:, S3 * order[j]:S3 * order[j] + M]
+    let3 = lambda j: T.rw3[:, S3 * order[j] + M:S3 * order[j] + M + 24]
+    raw4 = lambda j: T.rw4[:, M * order[j]:M * (order[j] + 1)]
+    col = lambda base, q: T.gt[:, base + M * q:base + M * (q + 1)]
+    l3of = lambda j: T.l3[:, 24 * j:24 * j + 24]
+    l4of = lambda j: T.l4[:, 24 * order[j]:24 * order[j] + 24]
+    l5of = lambda q: T.l5[:, 24 * q:24 * q + 24]
+    half = lambda b, t, hh, w: b[:, w * (2 * t + hh):w * (2 * t + hh + 1)]
+    mk4, mk5 = T.mk[:, 0:M], T.mk[:, M:2 * M]
     x3, x4, x5 = T.xf[:, 0:M], T.xf[:, M:2 * M], T.xf[:, 2 * M:3 * M]
-    tt(x4, T.h[:].indirect(T.lp[:]), mk4, A.mult, ["h", "lp", "mk4"], ["x4"])
-    fold(T.pc[:, 0:24], "pc", T.z, "z", lambda i: T.xf[:, M + i:2 * M:16], "x4")
+    pc, pgr = T.pf[:, 1:2], T.pf[:, 2:3]
+    fl = dict(allow_small_or_imprecise_dtypes=True)
+    g23 = ["x3in", "g2"] + ["g3_%d" % j for j in range(4)]
+    g24 = g23 + ["x4in"] + ["g4_%d" % j for j in range(4)]
+    g25 = g24 + ["g5_%d" % j for j in range(N)]
+    step = {}
 
-    def level3(q):
-        tt(T.gt[:, C3 + M * q:C3 + M * (q + 1)], T.h[:].indirect(l3of(q)),
-           T.st2[:, 16 + S2 * q:16 + S2 * q + M], A.max,
-           ["h", "l23_%d" % q, "own2a" if q == r else "st2"], ["g3_%d" % q])
+    writer["st1"] = [("r1", n_off * len(peers + others) + n_on)]
+    writer["l5own"] = [("r5", n_off * len(peers))]
+    writer["l5in"] = writer["l5own"] + [("q5", n_off * len(others) + n_on // 2)]
+    for j in range(1, 4):
+        writer["r3_%d" % j] = writer["c3_%d" % j] = [("a3%d" % order[j], n_off)]
+        writer["r4_%d" % j] = [("a4%d" % order[j], n_off)]
+        writer["l4_%d" % j] = [("al4", n_off * len(peers))]
+    for d in (3, 4):
+        writer["x%din" % d] = [("x%d" % d, sum(n for c in calls(d).values() for x, m, n in c))]
 
-    def decode_ln(a, n, src, rd, key):
-        act(T.ygs[:, a:a + n], src, F.Ln, rd, [key])
+    step["t12"] = lambda: load("t12", T.t12[:], T.tri[:, 0:40])
+    step["tb3"] = lambda: load("tb3", T.tb[:, 0:M], T.tri[:, 34:34 + M])
+    step["tb4"] = lambda: load("tb4", T.tb[:, M:2 * M], T.tri[:, 34 + M:34 + 2 * M])
+    step["pr"] = lambda: load("pr", T.pr[:], T.par[:])
+    step["ltz"] = lambda: fill(T.lt[:], "ltz", 0)
+    step["lt"] = lambda: load("lt", T.lt[0::16, :], T.let[:, 0:416], ["ltz"])
+    for t in range(8):
+        step["tx%d" % t] = lambda t=t: load("tx%d" % t, T.tx[:, 64 * t:64 * t + 64], T.txt[:, 1024 * t:1024 * t + 1024])
 
-    def decode_round(a, n, key):
-        act(T.ygs[:, a:a + n], T.ygs[:, a:a + n], F.Identity, [], [key], bias=MID + MAGIC, scale=K)
+    step["pi0"] = lambda: iota(T.pi[:, 0:1], [[1, 1]], 0, 1, "pi0")
+    step["nfa"] = lambda: iota(T.nf[:, 0:32], [[1, 32]], 288 + N * M + M * r, 0, "nfa", **fl)
+    step["nfb"] = lambda: iota(T.nf[:, 32:M], [[1, M - 32]], 288 + N * M + M * r + 32, 0, "nfb", **fl)
+    step["n5"] = lambda: iota(T.n5[:], [[1, M]], 288 + 2 * N * M + M * r, 0, "n5")
+    step["xio"] = lambda: iota(T.xio[:], [[1, 144]], -15, 0, "xio", **fl)
+    step["nea"] = lambda: enc(T.ne[:, 0:32], T.nf[:, 0:32], ["nfa"], ["nea"])
+    step["neb"] = lambda: enc(T.ne[:, 32:M], T.nf[:, 32:M], ["nfb"], ["neb"])
+    step["w3a"] = lambda: fill(T.w3[:, 0:1024], "w3a")
+    step["w3b"] = lambda: fill(T.w3[:, 1024:4096], "w3b")
 
-    def decode_end(a, n, key):
-        act(T.ygs[:, a:a + n], T.ygs[:, a:a + n], F.Identity, [], [key], bias=-MAGIC)
+    def pf():
+        for k, low in enumerate([15, 112]):
+            ts(T.pi[:, 1 + k:2 + k], T.pi[:, 0:1], low, None, A.bitwise_and, None, ["pi0"], ["pi%d" % (k + 1)])
+        cp(T.pf[:, 1:3], T.pi[:, 1:3], ["pi1", "pi2"], ["pf"])
 
-    tt(T.xw[:], T.h[:].indirect(T.c01u[:]), tmk(2), A.mult, ["h", "c01u", "tm2_0", "tm2_1"], ["xw"])
-    act(T.f4[:], T.pc[:, 0:24], F.Ln, [], ["pc", "f4"])
-    act(T.hc[:], T.h[:].indirect(T.l34[:]), F.Copy, ["h", "l34"], ["hc"])
-    fold(T.pe[:, 0:64], "pe", T.z, "z", lambda i: T.xw[:, i::16], "xw")
-    ts(T.f4r[:], T.f4[:], K / M, (MID - 288 - 191.5) / M, A.mult, A.add, ["f4"], ["f4r"])
-    ts(T.f4b[:], T.f4[:], K / X2, (MID - 288 + 16) / X2, A.mult, A.add, ["f4"], ["f4b"])
-    tt(T.f4b[:], T.f4b[:], T.f4r[:], A.add, ["f4r"], ["f4b"])
-    ts(T.f4u[:], T.f4b[:], float(X2), None, A.mult, None, ["f4b"], ["f4u"])
-    act(x3, T.ex[:].indirect(l3of(r)), F.Copy, ["ex", "l23_%d" % r], ["x3"])
-    act(T.ls[:, 64:128], T.pe[:, 0:64], F.Ln, [], ["pe", "ls2_0", "ls2_1"])
-    act(T.xw[:], T.ex[:].indirect(T.c01u[:]), F.Copy, ["ex", "c01u"], ["xw"])
-    fold(T.pe[:, 0:64], "pe", T.z, "z", lambda i: T.xw[:, i::16], "xw")
-    tt(T.o4[:], T.h[:].indirect(T.l34[:]), T.e4[:], A.max, ["h", "l34", "e4"], ["o4"])
-    level3(r)
+    def lab():
+        ts(T.la[:], T.xio[:, 15:31], 32.0, pc, A.mult, A.add, ["xio", "pf"], ["la"])
+        ts(T.pf[:, 8:9], pc, 32.0, 16.0, A.mult, A.add, ["pf"], ["pf8"])
+        ts(T.jl[:, 0:16], T.xio[:, 15:31], 32.0, 16.0, A.mult, A.add, ["xio"], ["jl0"])
+        ts(T.lb[:], T.xio[:, 0:16], 0.0, T.pf[:, 8:9], A.mult, A.add, ["xio", "pf8"], ["lb"])
 
-    tt(slot4(r), T.st2[:].indirect(T.f4u[:]), T.o4[:], A.max, ["st2", "f4u", "o4"], ["own4"])
-    spread(3, slot4(r), ["own4"])
-    tt(T.d4[:], T.st2[:].indirect(T.f4u[:]), T.hc[:], A.max, ["st2", "f4u", "hc"], ["d4"])
-    tt(x5, T.d4[:].indirect(T.pru[:, 50:74]), mk5, A.mult, ["d4", "pru", "mk5"], ["x5"])
-    fold(T.pd[:, 0:24], "pd", T.z, "z", lambda i: T.xf[:, 2 * M + i:3 * M:16], "x5")
-    decode_ln(34, M, T.gt[:, C3 + M * r:C3 + M * (r + 1)], ["g3_%d" % r], "yg3")
-    act(T.ls[:, 0:64], T.pe[:, 0:64], F.Ln, [], ["pe", "ls1_0", "ls1_1"])
-    decode_ln(34 + M, M, slot4(r), ["own4"], "yg4")
-    act(T.f5[:], T.pd[:, 0:24], F.Ln, [], ["pd", "f5"])
-    rest = [q for q in range(N) if q != r]
-    for q in rest:
-        letters(q, ["st2"])
-    level3(rest[0])
-    level3(rest[1])
-    ts(slot5(r), T.f5[:], K, MID - 32, A.mult, A.add, ["f5"], ["own5"])
-    spread(4, slot5(r), ["own5"])
-    hand_on(3, slot4)
-    hand_on(4, slot5)
-    writer["l5"] = writer["own5"] + arrivals(4)
-    writer["g4"] = writer["own4"] + arrivals(3)
+    def blk():
+        iota(T.bio[:], [[16, 8], [0, 16]], 0, 0, "bio", **fl)
+        ts(T.blk[:], T.bio[:], pgr, None, A.is_equal, None, ["bio", "pf"], ["blk"])
 
-    for q in range(N):
-        act(T.gt[:, 32 * q:32 * q + 32], T.h[:].indirect(l2of(q)), F.Copy, ["h", "l23_%d" % q], ["g2_%d" % q])
-    tmask(4)
-    tmask(5)
-    ts(T.off[:], T.ls[:, 64:128], K, MID - 32, A.mult, A.add, ["ls2_0", "ls2_1"], ["off0", "off1"])
-    for q in rest[2:]:
-        level3(q)
+    step["pf"], step["lab"], step["blk"] = pf, lab, blk
+    step["z"] = lambda: ts(T.z[:], T.xio[:], pgr, None, A.is_equal, None, ["xio", "pf"], ["z"])
+    step["zc"] = lambda: ts(T.z0[:], T.z[:], T.idn[:, 0:1], None, A.mult, None, ["z", "idn"], ["z0"])
+    step["z01"] = lambda: ts(T.z1[:], T.z[:], T.idn[:, 1:2], None, A.mult, None, ["z", "idn"], ["z1"])
+    step["lo1"] = lambda: cp(T.lo[:, 1:4:2], T.xio[:, 15:17], ["xio"], ["lo1"])
+    step["idn"] = lambda: ts(T.idn[:], T.xio[:, 15:31], pc, None, A.is_equal, None, ["xio", "pf"], ["idn"])
+    step["jl1"] = lambda: ts(T.jl[:, 16:32], T.xio[:, 0:16], 0.0, pc, A.mult, A.add, ["xio", "pf"], ["jl1"])
+    step["idr"] = lambda: act(T.idr[:], T.idn[:].indirect(T.jl[:, 16:32]), F.Copy, ["idn", "jl1"], ["idr"])
+
+    def own1():
+        ts(T.lo[:, 0:4:2], T.t12[:, 0:2], float(2 - 32 - 32 * r), None, A.add, None, ["t12"], ["lo0"])
+        cp(T.f48[:], T.t12[:].indirect(T.lo[:]), ["t12", "lo0", "lo1"], ["f48"])
+        enc(slot1, T.f48[:], ["f48"], ["own1"])
+
+    step["own1"] = own1
+    step["send1"] = lambda: send(slot1, ["own1"], off(peers + others, "r1"))
+    step["send1m"] = lambda: send(slot1, ["own1"], near(mate, "r1"))
+
+    step["tbf3"] = lambda: cp(T.tbf[:, 0:M], T.tb[:, 0:M], ["tb3"], ["tbf3"])
+    step["enc3"] = lambda: enc(raw3(0), T.tbf[:, 0:M], ["tbf3"], ["r3_0"])
+    step["tbf4"] = lambda: cp(T.tbf[:, M:2 * M], T.tb[:, M:2 * M], ["tb4"], ["tbf4"])
+    step["enc4"] = lambda: enc(raw4(0), T.tbf[:, M:2 * M], ["tbf4"], ["r4_0"])
+    step["pru"] = lambda: cp(T.pru[:], T.pr[:], ["pr"], ["pru"])
+
+    def y3():
+        ts(T.l16[:], T.lt[:, 0:32], 16.0, None, A.mult, None, ["lt"], ["l16"])
+        tt(T.y3[:], T.l16[:].indirect(T.pru[:, 2:26]), T.lt[:, 32:416], A.add, ["l16", "pru", "lt"], ["y3"])
+
+    step["y3"] = y3
+    step["fy3"] = lambda: fold("pc", 0, 24, "z0", lambda i: T.y3[:, i::16], ["y3"], "fy3")
+    step["l3own"] = lambda: cp(let3(0), T.pc[:, 0:24], ["fy3"], ["pc", "c3_0"])
+    step["send3"] = lambda: send(T.rw3[:, S3 * me:S3 * me + M + 24], ["r3_0", "c3_0"], off(peers, "a3%d" % me))
+    step["send4h"] = lambda: send(raw4(0), ["r4_0"], near(helpers[place], "hs"))
+    step["yp"] = lambda: act(T.yp[:], T.y3[:].indirect(T.pru[:, 26:50]), F.Copy, ["y3", "pru"], ["yp"])
+    step["fyp"] = lambda: fold("pd", 0, 24, "z0", lambda i: T.yp[:, i::16], ["yp"], "fyp")
+    step["lp"] = lambda: cp(T.lp[:], T.pd[:, 0:24], ["fyp"], ["pd", "lp"])
+    step["mk4"] = lambda: tt(mk4, raw3(0).indirect(T.pru[:, 26:50]), T.ne[:], A.is_equal,
+                             ["r3_0", "pru", "nea", "neb"], ["mk4"])
+    step["mk5"] = lambda: tt(mk5, T.tb[:, M:2 * M].indirect(T.pru[:, 50:74]), T.n5[:], A.is_equal,
+                             ["tb4", "pru", "n5"], ["mk5"])
+    step["yg1"] = lambda: act(T.ygs[:, 0:2], T.st1[:, S1 * r + 16:S1 * r + 64:32], F.Ln, ["own1"], ["yg1"])
+
+    def words():
+        x = lambda u: T.tx[:, 64 * u:64 * u + 64]
+        ts(T.c01[:], x(0), 16.0, None, A.mult, None, ["tx0"], ["c0"])
+        ts(T.w2[:], x(2), 256.0, None, A.mult, None, ["tx2"], ["w0"])
+        tt(T.c01[:], T.c01[:], x(1), A.add, ["tx1", "c0"], ["c01"])
+        tt(T.w2[:], T.w2[:], T.c01[:], A.add, ["c01", "w0"], ["w2"])
+        cp(T.w2u[:], T.w2[:], ["w2"], ["w2u"])
+
+    def yf0():
+        fill(T.yf0[:, 0:2], "yf0a")
+        ts(T.yf0[:, 2:34], T.lt[:, 0:32], 16.0, None, A.add, None, ["lt"], ["yf0b"])
+
+    step["words"], step["yf0"] = words, yf0
+    for t in range(3, 8):
+        step["txu%d" % t] = lambda t=t: cp(T.txu[:, 64 * t:64 * t + 64], T.tx[:, 64 * t:64 * t + 64], ["tx%d" % t],
+                                           ["txu%d" % t])
+
+    def tmask(t, hh):
+        copy("tm%d%s" % (t, "ab"[hh]), half(T.tm, t - 3, hh, 512), T.idn[:].indirect(half(T.txu, t, hh, 32)),
+             ["idn", "txu%d" % t], ["tm%d_%d" % (t, hh)])
+
+    step["t1r"] = lambda: act(T.t1r[:], T.st1[:].indirect(T.lb[:]), F.Copy, ["own1", "st1", "lb"], ["t1r"])
+    step["h"] = lambda: tt(T.h[:], T.st1[:].indirect(T.la[:]), T.t1r[:], A.max, ["own1", "st1", "la", "t1r"], ["h"])
+
+    def w3(row, src, key):
+        before("y", [key, "w3a", "w3b"], [])
+        Y.dma_start(T.w3[row::16, :], src).then_inc(T.sem.iw, 16)
+        writer["w3_%d" % row] = [("iw", 32)]
+
+    def g2():
+        tolist(T.l2[:], T.n2[:], ["n2l"], ["l2"])
+        cp(T.gt[:, 0:256].indirect(T.l2[:]), T.h[:], ["h", "l2"], ["g2"])
+
+    step["w3"], step["w3n"], step["g2"] = lambda: w3(0, T.h[:], "h"), lambda: w3(1, T.n2r[:], "n2c"), g2
+    step["n2l"] = lambda: act(T.n2[:], T.t1r[:, 0:16], F.Ln, ["t1r"], ["n2l"])
+    step["ex"] = lambda: tt(T.ex[:], T.st1[:].indirect(T.jl[:, 0:16]), T.idr[:], A.mult,
+                            ["own1", "st1", "jl0", "idr"], ["ex"])
+    step["n2r"] = lambda: op("p", lambda: P.matmul(T.ph[:, 64:320], T.blk[:], T.ex[:], True, True), ["blk", "ex"],
+                             ["ph", "n2r"])
+    step["n2c"] = lambda: act(T.n2r[:], T.ph[:, 64:320], F.Copy, ["n2r"], ["ph", "n2c"])
+    step["s2"] = lambda: copy("s2", T.xw[:], T.w3[:].indirect(T.w2u[:]), ["w3_0", "w3_1", "w2u"], ["xw"])
+    step["fs2"] = lambda: fold("pe", 0, 64, "z0", lambda i: T.xw[:, i::16], ["xw"], "fs2")
+    step["ls2"] = lambda: act(T.ls[:, 64:128], T.pe[:, 0:64], F.Ln, ["fs2"], ["pe", "ls2"])
+    step["fs1"] = lambda: fold("ph", 0, 64, "z1", lambda i: T.xw[:, i::16], ["xw"], "fs1")
+    step["ls1"] = lambda: act(T.ls[:, 0:64], T.ph[:, 0:64], F.Ln, ["fs1"], ["ph", "ls1"])
+    step["off3"] = lambda: tolist(T.off[:, 0:64], T.ls[:, 64:128], ["ls2"], ["off3_0", "off3_1"])
+
+    step["x4"] = lambda: tt(x4, T.h[:].indirect(T.lp[:]), mk4, A.mult, ["h", "lp", "mk4"], ["x4"])
+    step["fx4"] = lambda: fold("pc", 32, 24, "z", lambda i: T.xf[:, M + i:2 * M:16], ["x4"], "fx4")
+    step["f4"] = lambda: act(T.f4[:], T.pc[:, 32:56], F.Ln, ["fx4"], ["pc", "f4"])
+    step["l4own"] = lambda: tolist(l4of(0), T.f4[:], ["f4"], ["l4_0"])
+    step["sl4"] = lambda: send(l4of(0), ["l4_0"], off(peers, "al4"))
+    step["xp"] = lambda: act(T.xp[:], x4.indirect(T.pru[:, 50:74]), F.Copy, ["x4", "pru"], ["xp"])
+    step["fxp"] = lambda: fold("pd", 24, 24, "z", lambda i: T.xp[:, i::16], ["xp"], "fxp")
+    step["fp"] = lambda: act(T.fp[:], T.pd[:, 24:48], F.Ln, ["fxp"], ["pd", "fp"])
+    step["f4p"] = lambda: tolist(T.f4p[:], T.fp[:], ["fp"], ["f4p"])
+    step["x5"] = lambda: tt(x5, T.gt[:, 0:C4].indirect(T.f4p[:]), mk5, A.mult, g23 + ["f4p", "mk5"], ["x5"])
+    step["fx5"] = lambda: fold("pc", 64, 24, "z", lambda i: T.xf[:, 2 * M + i:3 * M:16], ["x5"], "fx5")
+    step["f5"] = lambda: act(T.f5[:], T.pc[:, 64:88], F.Ln, ["fx5"], ["pc", "f5"])
+    step["own5"] = lambda: tolist(l5of(r), T.f5[:], ["f5"], ["own5"])
+    step["sl5"] = lambda: send(l5of(r), ["own5"], off(peers, "r5"), near(helpers[place], "h5", on_eng[:n_on // 2]),
+                               near(mate, "q5", on_eng[n_on // 2:]))
+
+    def under4(j):
+        if "f" in var["sx4_%d" % j]:
+            act(T.d4[:, M * j:M * (j + 1)], T.gt[:, 0:C4].indirect(l4of(j)), F.Copy, g23 + ["l4_%d" % j], ["d4_%d" % j])
+
+    def part(base, d):
+        def of(x):
+            if "f" in var["sx%d_%d" % (d, x)]:
+                return col(base, rank_of(x)), ["d4_%d" % x, "r4_%d" % x], [T.d4[:, M * x:M * (x + 1)], raw4(x)]
+            return col(base, rank_of(x)), ["g%d_%d" % (d, x)], [col(base, rank_of(x))]
+        return of
+
+    def level5(j):
+        q = rank_of(j) if j < 4 else 2 * order[j - 4] + 1 - place
+        copy("l5_%d" % j, col(C5, q), T.gt[:, 0:C5].indirect(l5of(q)), g24 + ["own5", "l5own" if j < 4 else "l5in"],
+             ["g5_%d" % j])
+
+    for j in range(4):
+        step["lc_%d" % j] = lambda j=j: cp(l3of(j), let3(j), ["c3_%d" % j], ["l3_%d" % j])
+        step["lev3_%d" % j] = lambda j=j: tt(col(C3, rank_of(j)), T.h[:].indirect(l3of(j)), raw3(j), A.max,
+                                             ["h", "l3_%d" % j, "r3_%d" % j], ["g3_%d" % j])
+        step["lev4_%d" % j] = lambda j=j: tt(col(C4, rank_of(j)), T.gt[:, 0:C4].indirect(l4of(j)), raw4(j),
+                                             A.max, g23 + ["l4_%d" % j, "r4_%d" % j], ["g4_%d" % j])
+        step["d4_%d" % j] = lambda j=j: under4(j)
+        step["sx3_%d" % j] = lambda j=j: pieces(3, j, part(C3, 3))
+        step["sx4_%d" % j] = lambda j=j: pieces(4, j, part(C4, 4))
+    for j in range(N):
+        step["l5_%d" % j] = lambda j=j: level5(j)
+
+    step["x3"] = lambda: act(x3, T.ex[:].indirect(l3of(0)), F.Copy, ["ex", "l3_0"], ["x3"])
     for d in range(3):
-        fold(T.pg[:, 24 * d:24 * d + 24], "pg", T.z, "z",
-             lambda i: T.xf[:, M * d + 24 * i:M * d + 24 * (i + 1)], "x%d" % (d + 3))
-    act(T.yfl[:], T.pg[:, 0:72], F.Ln, [], ["pg", "yfl"])
-    writer["yg24"] = writer["yg2"] + writer["yg3"] + writer["yg4"]
+        step["fyf%d" % (d + 3)] = lambda d=d: fold("pg", 24 * d, 24, "z",
+                                                   lambda i: T.xf[:, M * d + 24 * i:M * d + 24 * (i + 1)],
+                                                   ["x%d" % (d + 3)], "fyf%d" % (d + 3))
+    step["yg2"] = lambda: act(T.ygs[:, 2:34], T.gt[:, 32 * r:32 * r + 32], F.Ln, ["g2"], ["yg2"])
+    step["yg3"] = lambda: act(T.ygs[:, 34:34 + M], col(C3, r), F.Ln, ["g3_0"], ["yg3"])
+    step["yg4"] = lambda: act(T.ygs[:, 34 + M:802], col(C4, r), F.Ln, ["g4_0"], ["yg4"])
+    step["yg5"] = lambda: act(T.ygs[:, 802:1186], col(C5, r), F.Ln, ["g5_0"], ["yg5"])
 
-    xs, ps = [T.xa, T.xb], [T.pa, T.pb]
-    g3keys = ["g2_%d" % q for q in range(N)] + ["g3_%d" % q for q in range(N)]
-    g5keys = ["g5_%d" % k for k in range(6)]
+    def rnd(q, ap, rd, key):
+        if q == "v":
+            ts(ap, ap, K, MID + MAGIC, A.mult, A.add, rd, [key])
+        else:
+            act(ap, ap, F.Identity, rd, [key], bias=MID + MAGIC, scale=K)
+
+    def sub(q, out, ap, rd, key):
+        if q == "v":
+            ts(out, ap, -MAGIC, None, A.add, None, rd, [key])
+        else:
+            act(out, ap, F.Identity, rd, [key], bias=-MAGIC)
+
+    def yg_out(nm, a, b):
+        sub(var["sb" + nm], T.ygs[:, a:b], T.ygs[:, a:b], ["rn" + nm], "sb" + nm)
+        store("y", T.yg[:, a:b], T.ygs[:, a:b], ["sb" + nm, "x4in", "l5in"])
+
+    for nm, a, b, rd in (("A", 0, 418, ["yg1", "yg2", "yg3"]), ("B", 418, 802, ["yg4"]), ("C", 802, 1186, ["yg5"])):
+        step["rn" + nm] = lambda nm=nm, a=a, b=b, rd=rd: rnd(var["rn" + nm], T.ygs[:, a:b], rd, "rn" + nm)
+        step["sb" + nm] = lambda nm=nm, a=a, b=b: yg_out(nm, a, b)
+
+    def yfl():
+        act(T.yfl[:], T.pg[:, 0:72], F.Ln, ["fyf3", "fyf4", "fyf5"], ["pg", "yfl0"])
+        rnd(var["yfl"], T.yfl[:], ["yfl0"], "yfl1")
+        sub(var["yfl"], T.yfl[:], T.yfl[:], ["yfl1"], "yfl")
+        store("y", T.yf[:, 0:34], T.yf0[0::16, :], ["yf0a", "yf0b", "x4in", "l5in"])
+        for d in range(3):
+            store("y", T.yf[:, 34 + M * d:34 + M * (d + 1)], T.yfl[:, 24 * d:24 * d + 24], ["yfl"])
+
+    step["yfl"] = yfl
+
+    whole = lambda t: var["look%da" % t] == "F"
+    bank_of = lambda t, hh: "pa" if (t % 2 if whole(t) else hh == 0) else "pb"
 
     def lsout(t, hh):
-        return T.ol[:, 32 * hh:32 * hh + 32] if t == 7 else T.ls[:, 64 * (t - 1) + 32 * hh:64 * (t - 1) + 32 * hh + 32]
+        return half(T.ol, hh, 0, 32) if t == 7 else half(T.ls, t - 1, hh, 32)
 
     def look(t, hh):
-        top, keys = (C4, g3keys) if t == 3 else (C5, g3keys + ["g4"]) if t == 4 else (CW, g3keys + ["g4"] + g5keys)
-        tt(xs[hh][:], T.gt[:, 0:top].indirect(T.off[:, 32 * hh:32 * hh + 32]), tmk(t, 32 * hh, 32 * hh + 32), A.mult,
-           keys + ["off%d" % hh, "tm%d_%d" % (t, hh)], ["x_%d" % hh])
-        fold(ps[hh][:, 0:32], "ps%d" % hh, T.z, "z", lambda i: xs[hh][:, i::16], "x_%d" % hh)
+        top, keys = (C4, g23) if t == 3 else (C5, g24) if t == 4 else (CW, g25)
+        if whole(t) and hh:
+            return
+        hs = [0, 1] if whole(t) else [hh]
+        n, a = 32 * len(hs), 64 * (t - 3) + 32 * hh
+        tt(T.xs[:, 16 * a:16 * (a + n)], T.gt[:, 0:top].indirect(T.off[:, a:a + n]), T.tm[:, 16 * a:16 * (a + n)],
+           A.mult, keys + ["off%d_%d" % (t, x) for x in hs] + ["tm%d_%d" % (t, x) for x in hs], ["x%d_%d" % (t, hh)])
+        fold(bank_of(t, hh), a, n, "z", lambda i: T.xs[:, 16 * a + i:16 * (a + n):16], ["x%d_%d" % (t, hh)],
+             "fx%d_%d" % (t, hh))
 
     def ln(t, hh):
-        act(lsout(t, hh), ps[hh][:, 0:32], F.Ln, [], ["ps%d" % hh, "ls%d_%d" % (t, hh)])
+        bank, a = bank_of(t, hh), 64 * (t - 3)
+        if whole(t) and t != 7:
+            if hh == 0:
+                act(T.ls[:, 64 * (t - 1):64 * t], T[bank][:, a:a + 64], F.Ln, ["fx%d_0" % t],
+                    [bank, "ls%d_0" % t, "ls%d_1" % t])
+            return
+        act(lsout(t, hh), T[bank][:, a + 32 * hh:a + 32 * hh + 32], F.Ln, ["fx%d_%d" % (t, 0 if whole(t) else hh)],
+            [bank, "ls%d_%d" % (t, hh)])
 
     def nxt(t, hh):
-        ts(T.off[:, 32 * hh:32 * hh + 32], lsout(t, hh), K, MID - 32, A.mult, A.add,
-           ["ls%d_%d" % (t, hh)], ["off%d" % hh])
+        u = t - 1
+        if whole(u):
+            if hh == 0:
+                tolist(T.off[:, 64 * (t - 3):64 * (t - 2)], T.ls[:, 64 * (u - 1):64 * u], ["ls%d_0" % u, "ls%d_1" % u],
+                       ["off%d_0" % t, "off%d_1" % t])
+            return
+        tolist(half(T.off, t - 3, hh, 32), lsout(u, hh), ["ls%d_%d" % (u, hh)], ["off%d_%d" % (t, hh)])
 
     def most(t):
-        tt(T.mx[:], T.mx[:], T.ls[:, 64 * (t - 1):64 * t], A.max, ["ls%d_0" % t, "ls%d_1" % t], ["mx"])
+        tt(T.mx[:], T.mx[:], T.ls[:, 64 * (t - 1):64 * t], A.max, ["mx0", "ls%d_0" % t, "ls%d_1" % t],
+           ["mx", "mx%d" % t])
 
-    look(3, 0)
-    look(3, 1)
-    ts(T.ygs[:, 2:802], T.ygs[:, 2:802], K, MID + MAGIC, A.mult, A.add, [], ["yg24"])
-    ln(3, 0)
-    decode_end(2, 800, "yg24")
-    ln(3, 1)
-    ts(T.yfl[:], T.yfl[:], K, MID + MAGIC, A.mult, A.add, [], ["yfl"])
-    tt(T.mx[:], T.ls[:, 0:64], T.ls[:, 64:128], A.max, ["ls1_0", "ls1_1", "ls2_0", "ls2_1"], ["mx"])
-    ts(T.yfl[:], T.yfl[:], -MAGIC, None, A.add, None, [], ["yfl"])
-    nxt(3, 0)
+    def mx():
+        tt(T.mx[:], T.ls[:, 0:64], T.ls[:, 64:128], A.max, ["ls1", "ls2"], ["mx0", "mx"])
+        most(3)
 
-    def level5(q, k):
-        out = T.gt[:, C5 + 512 * k:C5 + 512 * (k + 1)]
-        src = T.gt[:, 0:C5].indirect(T.l5[:, 32 * k:32 * k + 32])
-        rd = g3keys + ["g4", "l5"]
-        if q == "a":
-            act(out, src, F.Copy, rd, ["g5_%d" % k])
-        else:
-            cp(out, src, rd, ["g5_%d" % k])
+    def end(hh):
+        tt(half(T.ol, hh, 1, 32), half(T.mx, 0, hh, 32), half(T.ol, hh, 0, 32), A.max,
+           ["mx", "mx4", "mx5", "mx6", "ls7_%d" % hh], ["ol0_%d" % hh])
+        rnd("v", T.ol[:, 64 * hh:64 * hh + 64], ["ol0_%d" % hh], "ol1_%d" % hh)
+        sub("v", half(T.oo, 0, hh, 32), half(T.ol, hh, 0, 32), ["ol1_%d" % hh], "ol2_%d" % hh)
+        sub("a", half(T.oo, 1, hh, 32), half(T.ol, hh, 1, 32), ["ol1_%d" % hh], "ol3_%d" % hh)
 
-    look(4, 0)
-    store("y", T.yg[:, 0:802], T.ygs[:, 0:802], ["yg1", "yg24", "g4"])
-    store("y", T.yf[:, 0:34], T.yf0[:], ["yf0a", "yf0b"])
-    for d in range(3):
-        store("y", T.yf[:, 34 + M * d:34 + M * (d + 1)], T.yfl[:, 24 * d:24 * d + 24], ["yfl"])
-    level5("a", 0)
-    nxt(3, 1)
-    look(4, 1)
-    most(3)
-    level5("a", 1)
-    level5("a", 2)
-    level5("v", 4)
-    ln(4, 0)
-    level5("v", 5)
-    level5("a", 3)
-    ln(4, 1)
-    nxt(4, 0)
-    look(5, 0)
-    nxt(4, 1)
-    tmask(6, 0, 32)
-    decode_ln(802, M, T.gt[:, C5 + M * r:C5 + M * (r + 1)], g5keys, "yg5")
-    look(5, 1)
-    decode_round(802, M, "yg5")
-    most(4)
-    ln(5, 0)
-    tmask(6, 32, 64)
-    nxt(5, 0)
-    look(6, 0)
-    ln(5, 1)
-    tmask(7, 0, 32)
-    nxt(5, 1)
-    look(6, 1)
-    most(5)
-    ln(6, 0)
-    tmask(7, 32, 64)
-    nxt(6, 0)
-    look(7, 0)
-    ln(6, 1)
-    decode_end(802, M, "yg5")
-    store("y", T.yg[:, 802:1186], T.ygs[:, 802:1186], ["yg5"])
-    nxt(6, 1)
-    look(7, 1)
-    most(6)
-    ln(7, 0)
-    ln(7, 1)
-    tt(T.ol[:, 64:128], T.mx[:], T.ol[:, 0:64], A.max, ["mx", "ls7_0", "ls7_1"], ["ol"])
-    ts(T.ol[:], T.ol[:], K, MID + MAGIC, A.mult, A.add, [], ["ol"])
-    ts(T.ol[:], T.ol[:], -MAGIC, None, A.add, None, [], ["ol"])
-    store("y", T.yl[:], T.ol[:, 0:64], ["ol"])
-    store("a", T.ym[:], T.ol[:, 64:128], ["ol"])
+    def end_b():
+        end(1)
+        store("y", T.yl[:], T.oo[:, 0:64], ["ol2_0", "ol2_1"])
+        store("a", T.ym[:], T.oo[:, 64:128], ["ol3_0", "ol3_1"])
+
+    for t in range(3, 8):
+        for hh in range(2):
+            for name, fn in (("tm", tmask), ("look", look), ("ln", ln), ("nxt", nxt)):
+                step["%s%d%s" % (name, t, "ab"[hh])] = lambda fn=fn, t=t, hh=hh: fn(t, hh)
+        step["most%d" % t] = lambda t=t: most(t)
+    step["mx"], step["enda"], step["endb"] = mx, lambda: end(0), end_b
+
+    for name in ORDER:
+        step[name.partition(":")[0]]()
 
     wait("g", [("loc", loc[0])])
     wait("y", [("sv", count["v"]), ("sa", count["a"]), ("sp", count["p"]), ("sg", count["g"]), ("out", outs[0])])

from concourse.bass import DstId, RemoteDMATransfer
from concourse.mybir import AluOpType as A, ActivationFunctionType as F

N = 8
M = 384
D = 0.0092
K = 1.0 / D
MID = 4752.0
MAGIC = 12582912.0
S1 = 64
S3 = M + 32
C3, C4, C5, CW = 256, 256 + N * M, 256 + 2 * N * M, 256 + 3 * N * M
ORDER = """
t12:a pi0 nfa xio ltz:v pf tb4:y tx0:y tx5:y pr:a lt:y tb3:y tx7:y tx3:y tx6:y tx2:y tx4:y tx1:y nea lo1 lab idn own1
nfb z jl1 idr neb w3a yf0 pru zc y3 fy3 tbf3 tbf4 l3own yp enc4 enc3 fyp txu3 txu5 blk lc_0 words w3b mk4 send1 tm3a:a
yg1 send1m send4h send3 lp ex txu6 t1r h txu4 n2r x4 lc_1 lev3_1 fx4 n5 x3 n2c tm5a:a n2l f4 w3 w3n l4own lev3_0 lc_2
lev3_2 lc_3 z01 lev3_3 mk5 tm4b:a xp fxp s2:a tm3b:a fp sl4 sx3_1:n sx3_2:w sx3_3:w tm6a:a fs2 g2 f4p d4_3 ls2
sx4_3:fw txu7 x5 lev4_2 fx5 f5 off3 own5 lev4_0 lev4_1 tm4a:a yg2 fyf3 fs1 ls1 yg4 tm7b:a yg3 rnB:a tm7a:a fyf4
look3a:F ln3a rnA:a sl5 sx4_2:n sx4_1:w lev4_3 tm5b:v nxt4a mx look4a:F fyf5 l5_2:a l5_0:a l5_1:a l5_3:a ln4a l5_7:a
l5_5:v l5_6:v l5_4:v nxt5a look5a yg5 sbB:a sbA:a ln5a tm6b:a look5b nxt6a look6a ln5b ln6a nxt6b most5 look6b nxt7a
most4 look7a ln6b rnC:a sbC:a ln7a yfl:a nxt7b look7b ln7b most6 enda endb d4_1 d4_2 look3b ln3b nxt4b sx3_0:j d4_0
sx4_0:j ln4b nxt5b look4b
""".split()


def _bufs(where, dtype, **shapes):
    return {k: (where, [128, v] if isinstance(v, int) else v, dtype) for k, v in shapes.items()}


SCRATCH = {}
SCRATCH.update(_bufs("sbuf", "int32", t12=40, tb=2 * M, pr=74, tx=512, lt=416, l16=32, pi=8, n5=M))
SCRATCH.update(_bufs("sbuf", "uint16", l3=4 * 24, l4=4 * 24, l5=N * 24, pru=74, txu=512, w2u=64,
                     lo=4, l2=16, la=16, lb=16, lp=24, f4p=24, off=5 * 64, jl=32))
SCRATCH.update(_bufs("sbuf", "bfloat16", st1=N * S1, rw3=4 * S3, rw4=4 * M, d4=4 * M, gt=CW, z=144, z0=144, z1=144,
                     idn=16, blk=128, mk=2 * M, y3=M, yp=M, xp=M, h=256, t1r=256, xf=3 * M, tm=5 * 1024,
                     xs=5 * 1024, xw=1024, ex=256, n2r=256, idr=256, ne=M, w3=4096))
SCRATCH.update(_bufs("sbuf", "float32", tbf=2 * M, nf=M, f48=S1, yf0=34, pf=12, xio=144, n2=16, f4=24,
                     fp=24, f5=24, yfl=72, ls=6 * 64, mx=64, ol=128, oo=128, ygs=1186, c01=64, w2=64, bio=128))
SCRATCH.update(_bufs("psum", "float32", pa=512, pb=512, pc=512, pd=512, pe=512, pg=512, ph=512))
SEMAPHORES = (["sv", "sa", "sp", "sg", "loc", "out", "iw", "hs", "h5", "r1", "x3", "x4", "r5", "q5", "al4",
               "it12", "ilt", "itb3", "itb4", "ipr"] + ["itx%d" % t for t in range(8)]
              + ["%s%d" % (k, c) for k in ("a3", "a4") for c in range(4)])
OPT = {}


def rank_program(g, core, T, topo):
    cores = list(T.cores)
    chips = []
    for c in cores:
        if topo.chip(c) not in chips:
            chips.append(topo.chip(c))
    on = {ch: [c for c in cores if topo.chip(c) == ch] for ch in chips}
    mine = topo.chip(core)
    if mine not in chips:
        return
    me = chips.index(mine)
    to_chips = [chips[(me + k) % len(chips)] for k in range(1, len(chips))]
    from_chips = [chips[(me - k) % len(chips)] for k in range(1, len(chips))]
    helpers = [c for c in topo.cores_of(core) if topo.die(c) != topo.die(on[mine][0])
               and all(topo.may_write(c, d) for ch in to_chips for d in on[ch])]

    def dst(c):
        rid, pid, _se = topo.addr(c)
        return DstId(rid=rid, pnc=pid)

    r = T.rank_of(core)
    place = on[mine].index(core) if r is not None else helpers.index(core) if core in helpers[:2] else None
    if place is None:
        return
    peers = [on[ch][place] for ch in to_chips]
    others = [c for ch in to_chips for c in on[ch] if c not in peers]
    off_mask = topo.mask(core, peers[0])
    n_off = len(topo.engines(core, peers[0]))
    mate = [c for c in on[mine] if c != core][0]
    all_eng = topo.engines(core, mate)
    on_eng = [e for e in all_eng if e not in topo.engines(core, peers[0])]
    bits = lambda es: sum(1 << e for e in es)
    n_on = len(on_eng)
    if r is None:
        q = 2 * me + place
        for sem, n_in, ap, to, there in (("hs", n_on, T.rw4[:, M * me:M * (me + 1)], peers, "a4%d" % me),
                                         ("h5", n_on // 2, T.l5[:, 24 * q:24 * q + 24], others, "q5")):
            g.wait_ge(T.sem[sem], n_in)
            g.remote_dma_fused([RemoteDMATransfer(dst_ids=[dst(c) for c in to], dma_engine_mask=off_mask,
                                                  remote_sem=T.sem[there], srcs=[ap], dsts=[ap for c in to])],
                               local_sem=T.sem.loc)
        g.wait_ge(T.sem.loc, 2 * n_off)
        return
    assert r == 2 * me + place
    order = [me] + [chips.index(ch) for ch in from_chips]
    rank_of = lambda j: 2 * order[j] + place

    V, S, P, Y = g.vector, g.scalar, g.tensor, g.sync
    queue = {"v": V, "a": S, "p": P, "g": g, "y": Y}
    semof = {"v": "sv", "a": "sa", "p": "sp", "g": "sg"}
    count = {"v": 0, "a": 0, "p": 0, "g": 0}
    waited = {}
    writer = {}
    readers = {}
    loc = [0]
    outs = [0]
    var = dict(x.partition(":")[::2] for x in ORDER)

    def wait(q, hs):
        need = {}
        for s, n in hs:
            need[s] = max(need.get(s, 0), n)
        for s, n in need.items():
            if waited.get((q, s), 0) < n:
                queue[q].wait_ge(T.sem[s], n)
                waited[(q, s)] = n

    def before(q, rd, wr):
        hs = []
        for k in rd:
            hs += writer[k]
        for k in wr:
            hs += writer.get(k, []) + readers.get(k, [])
        wait(q, hs)

    def after(h, rd, wr):
        for k in rd:
            readers.setdefault(k, []).append(h)
        for k in wr:
            writer[k] = [h]
            readers[k] = []

    def op(q, fn, rd, wr):
        before(q, rd, wr)
        count[q] += 1
        fn().then_inc(T.sem[semof[q]], 1)
        after((semof[q], count[q]), rd, wr)

    def load(key, out, in_, rd=()):
        before(var[key], rd, [])
        queue[var[key]].dma_start(out, in_).then_inc(T.sem["i" + key], 16)
        writer[key] = [("i" + key, 16)]

    def store(q, out, in_, rd):
        before(q, rd, [])
        queue[q].dma_start(out, in_).then_inc(T.sem.out, 16)
        outs[0] += 16

    def send(ap, rd, *parts):
        before("g", rd, [])
        g.remote_dma_fused([RemoteDMATransfer(dst_ids=[dst(c) for c in cs], dma_engine_mask=m, remote_sem=T.sem[s],
                                              srcs=[ap], dsts=[ap for c in cs]) for cs, m, n, s in parts],
                           local_sem=T.sem.loc)
        loc[0] += sum(n for cs, m, n, s in parts)

    off = lambda cs, s: (cs, off_mask, n_off, s)
    near = lambda c, s, es=on_eng: ([c], bits(es), len(es), s)

    def calls(d):
        out, cur = {}, []
        for j in range(4):
            cur.append(j)
            if "j" not in var["sx%d_%d" % (d, j)] or j == 3:
                es = all_eng if "w" in var["sx%d_%d" % (d, j)] else on_eng
                n = len(es) // (4 if len(cur) > 2 else len(cur))
                out[j] = [(x, bits(es[n * i:n * i + n]), n) for i, x in enumerate(cur)]
                cur = []
        return out

    def pieces(d, j, part):
        if j in calls(d):
            before("g", sum([part(x)[1] for x, m, n in calls(d)[j]], []), [])
            g.remote_dma_fused([RemoteDMATransfer(dst_ids=[dst(mate)], dma_engine_mask=m, remote_sem=T.sem["x%d" % d],
                                                  srcs=part(x)[2], dsts=[part(x)[0]], alu_op=2 * (len(part(x)[2]) - 1))
                                for x, m, n in calls(d)[j]], local_sem=T.sem.loc)
            loc[0] += sum(n for x, m, n in calls(d)[j])

    def fold(bank, a, n, w, x, xkeys, key):
        before("p", [w] + xkeys, [bank])
        for i in range(16):
            ins = P.matmul(T[bank][:, a:a + n], T[w][:, 15 - i:143 - i], x(i), i == 0, i == 15)
        count["p"] += 1
        ins.then_inc(T.sem.sp, 1)
        after(("sp", count["p"]), [w] + xkeys, [bank, key])

    def ts(out, in0, s1, s2, o0, o1, rd, wr):
        if o1 is None:
            op("v", lambda: V.tensor_scalar(out, in0, s1, None, o0), rd, wr)
        else:
            op("v", lambda: V.tensor_scalar(out, in0, s1, s2, o0, o1), rd, wr)

    def tt(out, in0, in1, o, rd, wr):
        op("v", lambda: V.tensor_tensor(out, in0, in1, o), rd, wr)

    def cp(out, in_, rd, wr):
        op("v", lambda: V.tensor_copy(out, in_), rd, wr)

    def act(out, in_, f, rd, wr, bias=0.0, scale=1.0):
        op("a", lambda: S.activation(out, in_, f, bias=bias, scale=scale), rd, wr)

    def copy(name, out, in_, rd, wr):
        if var[name] == "v":
            cp(out, in_, rd, wr)
        else:
            act(out, in_, F.Copy, rd, wr)

    def enc(out, in_, rd, wr):
        act(out, in_, F.Exp, rd, wr, bias=-D * MID, scale=D)

    def tolist(out, in_, rd, wr):
        ts(out, in_, K, MID - 32, A.mult, A.add, rd, wr)

    def fill(ap, key, value=0.0):
        op("v", lambda: V.memset(ap, value), [], [key])

    def iota(out, pattern, base, mult, key, **kw):
        op("g", lambda: g.iota(out, pattern, base, mult, **kw), [], [key])

    slot1 = T.st1[:, S1 * r:S1 * (r + 1)]
    raw3 = lambda j: T.rw3[:, S3 * order[j]:S3 * order[j] + M]
    let3 = lambda j: T.rw3[:, S3 * order[j] + M:S3 * order[j] + M + 24]
    raw4 = lambda j: T.rw4[:, M * order[j]:M * (order[j] + 1)]
    col = lambda base, q: T.gt[:, base + M * q:base + M * (q + 1)]
    l3of = lambda j: T.l3[:, 24 * j:24 * j + 24]
    l4of = lambda j: T.l4[:, 24 * order[j]:24 * order[j] + 24]
    l5of = lambda q: T.l5[:, 24 * q:24 * q + 24]
    half = lambda b, t, hh, w: b[:, w * (2 * t + hh):w * (2 * t + hh + 1)]
    mk4, mk5 = T.mk[:, 0:M], T.mk[:, M:2 * M]
    x3, x4, x5 = T.xf[:, 0:M], T.xf[:, M:2 * M], T.xf[:, 2 * M:3 * M]
    pc, pgr = T.pf[:, 1:2], T.pf[:, 2:3]
    fl = dict(allow_small_or_imprecise_dtypes=True)
    g23 = ["x3in", "g2"] + ["g3_%d" % j for j in range(4)]
    g24 = g23 + ["x4in"] + ["g4_%d" % j for j in range(4)]
    g25 = g24 + ["g5_%d" % j for j in range(N)]
    step = {}

    writer["st1"] = [("r1", n_off * len(peers + others) + n_on)]
    writer["l5own"] = [("r5", n_off * len(peers))]
    writer["l5in"] = writer["l5own"] + [("q5", n_off * len(others) + n_on // 2)]
    for j in range(1, 4):
        writer["r3_%d" % j] = writer["c3_%d" % j] = [("a3%d" % order[j], n_off)]
        writer["r4_%d" % j] = [("a4%d" % order[j], n_off)]
        writer["l4_%d" % j] = [("al4", n_off * len(peers))]
    for d in (3, 4):
        writer["x%din" % d] = [("x%d" % d, sum(n for c in calls(d).values() for x, m, n in c))]

    step["t12"] = lambda: load("t12", T.t12[:], T.tri[:, 0:40])
    step["tb3"] = lambda: load("tb3", T.tb[:, 0:M], T.tri[:, 34:34 + M])
    step["tb4"] = lambda: load("tb4", T.tb[:, M:2 * M], T.tri[:, 34 + M:34 + 2 * M])
    step["pr"] = lambda: load("pr", T.pr[:], T.par[:])
    step["ltz"] = lambda: fill(T.lt[:], "ltz", 0)
    step["lt"] = lambda: load("lt", T.lt[0::16, :], T.let[:, 0:416], ["ltz"])
    for t in range(8):
        step["tx%d" % t] = lambda t=t: load("tx%d" % t, T.tx[:, 64 * t:64 * t + 64], T.txt[:, 1024 * t:1024 * t + 1024])

    step["pi0"] = lambda: iota(T.pi[:, 0:1], [[1, 1]], 0, 1, "pi0")
    step["nfa"] = lambda: iota(T.nf[:, 0:32], [[1, 32]], 288 + N * M + M * r, 0, "nfa", **fl)
    step["nfb"] = lambda: iota(T.nf[:, 32:M], [[1, M - 32]], 288 + N * M + M * r + 32, 0, "nfb", **fl)
    step["n5"] = lambda: iota(T.n5[:], [[1, M]], 288 + 2 * N * M + M * r, 0, "n5")
    step["xio"] = lambda: iota(T.xio[:], [[1, 144]], -15, 0, "xio", **fl)
    step["nea"] = lambda: enc(T.ne[:, 0:32], T.nf[:, 0:32], ["nfa"], ["nea"])
    step["neb"] = lambda: enc(T.ne[:, 32:M], T.nf[:, 32:M], ["nfb"], ["neb"])
    step["w3a"] = lambda: fill(T.w3[:, 0:1024], "w3a")
    step["w3b"] = lambda: fill(T.w3[:, 1024:4096], "w3b")

    def pf():
        for k, low in enumerate([15, 112]):
            ts(T.pi[:, 1 + k:2 + k], T.pi[:, 0:1], low, None, A.bitwise_and, None, ["pi0"], ["pi%d" % (k + 1)])
        cp(T.pf[:, 1:3], T.pi[:, 1:3], ["pi1", "pi2"], ["pf"])

    def lab():
        ts(T.la[:], T.xio[:, 15:31], 32.0, pc, A.mult, A.add, ["xio", "pf"], ["la"])
        ts(T.pf[:, 8:9], pc, 32.0, 16.0, A.mult, A.add, ["pf"], ["pf8"])
        ts(T.jl[:, 0:16], T.xio[:, 15:31], 32.0, 16.0, A.mult, A.add, ["xio"], ["jl0"])
        ts(T.lb[:], T.xio[:, 0:16], 0.0, T.pf[:, 8:9], A.mult, A.add, ["xio", "pf8"], ["lb"])

    def blk():
        iota(T.bio[:], [[16, 8], [0, 16]], 0, 0, "bio", **fl)
        ts(T.blk[:], T.bio[:], pgr, None, A.is_equal, None, ["bio", "pf"], ["blk"])

    step["pf"], step["lab"], step["blk"] = pf, lab, blk
    step["z"] = lambda: ts(T.z[:], T.xio[:], pgr, None, A.is_equal, None, ["xio", "pf"], ["z"])
    step["zc"] = lambda: ts(T.z0[:], T.z[:], T.idn[:, 0:1], None, A.mult, None, ["z", "idn"], ["z0"])
    step["z01"] = lambda: ts(T.z1[:], T.z[:], T.idn[:, 1:2], None, A.mult, None, ["z", "idn"], ["z1"])
    step["lo1"] = lambda: cp(T.lo[:, 1:4:2], T.xio[:, 15:17], ["xio"], ["lo1"])
    step["idn"] = lambda: ts(T.idn[:], T.xio[:, 15:31], pc, None, A.is_equal, None, ["xio", "pf"], ["idn"])
    step["jl1"] = lambda: ts(T.jl[:, 16:32], T.xio[:, 0:16], 0.0, pc, A.mult, A.add, ["xio", "pf"], ["jl1"])
    step["idr"] = lambda: act(T.idr[:], T.idn[:].indirect(T.jl[:, 16:32]), F.Copy, ["idn", "jl1"], ["idr"])

    def own1():
        ts(T.lo[:, 0:4:2], T.t12[:, 0:2], float(2 - 32 - 32 * r), None, A.add, None, ["t12"], ["lo0"])
        cp(T.f48[:], T.t12[:].indirect(T.lo[:]), ["t12", "lo0", "lo1"], ["f48"])
        enc(slot1, T.f48[:], ["f48"], ["own1"])

    step["own1"] = own1
    step["send1"] = lambda: send(slot1, ["own1"], off(peers + others, "r1"))
    step["send1m"] = lambda: send(slot1, ["own1"], near(mate, "r1"))

    step["tbf3"] = lambda: cp(T.tbf[:, 0:M], T.tb[:, 0:M], ["tb3"], ["tbf3"])
    step["enc3"] = lambda: enc(raw3(0), T.tbf[:, 0:M], ["tbf3"], ["r3_0"])
    step["tbf4"] = lambda: cp(T.tbf[:, M:2 * M], T.tb[:, M:2 * M], ["tb4"], ["tbf4"])
    step["enc4"] = lambda: enc(raw4(0), T.tbf[:, M:2 * M], ["tbf4"], ["r4_0"])
    step["pru"] = lambda: cp(T.pru[:], T.pr[:], ["pr"], ["pru"])

    def y3():
        ts(T.l16[:], T.lt[:, 0:32], 16.0, None, A.mult, None, ["lt"], ["l16"])
        tt(T.y3[:], T.l16[:].indirect(T.pru[:, 2:26]), T.lt[:, 32:416], A.add, ["l16", "pru", "lt"], ["y3"])

    step["y3"] = y3
    step["fy3"] = lambda: fold("pc", 0, 24, "z0", lambda i: T.y3[:, i::16], ["y3"], "fy3")
    step["l3own"] = lambda: cp(let3(0), T.pc[:, 0:24], ["fy3"], ["pc", "c3_0"])
    step["send3"] = lambda: send(T.rw3[:, S3 * me:S3 * me + M + 24], ["r3_0", "c3_0"], off(peers, "a3%d" % me))
    step["send4h"] = lambda: send(raw4(0), ["r4_0"], near(helpers[place], "hs"))
    step["yp"] = lambda: act(T.yp[:], T.y3[:].indirect(T.pru[:, 26:50]), F.Copy, ["y3", "pru"], ["yp"])
    step["fyp"] = lambda: fold("pd", 0, 24, "z0", lambda i: T.yp[:, i::16], ["yp"], "fyp")
    step["lp"] = lambda: cp(T.lp[:], T.pd[:, 0:24], ["fyp"], ["pd", "lp"])
    step["mk4"] = lambda: tt(mk4, raw3(0).indirect(T.pru[:, 26:50]), T.ne[:], A.is_equal,
                             ["r3_0", "pru", "nea", "neb"], ["mk4"])
    step["mk5"] = lambda: tt(mk5, T.tb[:, M:2 * M].indirect(T.pru[:, 50:74]), T.n5[:], A.is_equal,
                             ["tb4", "pru", "n5"], ["mk5"])
    step["yg1"] = lambda: act(T.ygs[:, 0:2], T.st1[:, S1 * r + 16:S1 * r + 64:32], F.Ln, ["own1"], ["yg1"])

    def words():
        x = lambda u: T.tx[:, 64 * u:64 * u + 64]
        ts(T.c01[:], x(0), 16.0, None, A.mult, None, ["tx0"], ["c0"])
        ts(T.w2[:], x(2), 256.0, None, A.mult, None, ["tx2"], ["w0"])
        tt(T.c01[:], T.c01[:], x(1), A.add, ["tx1", "c0"], ["c01"])
        tt(T.w2[:], T.w2[:], T.c01[:], A.add, ["c01", "w0"], ["w2"])
        cp(T.w2u[:], T.w2[:], ["w2"], ["w2u"])

    def yf0():
        fill(T.yf0[:, 0:2], "yf0a")
        ts(T.yf0[:, 2:34], T.lt[:, 0:32], 16.0, None, A.add, None, ["lt"], ["yf0b"])

    step["words"], step["yf0"] = words, yf0
    for t in range(3, 8):
        step["txu%d" % t] = lambda t=t: cp(T.txu[:, 64 * t:64 * t + 64], T.tx[:, 64 * t:64 * t + 64], ["tx%d" % t],
                                           ["txu%d" % t])

    def tmask(t, hh):
        copy("tm%d%s" % (t, "ab"[hh]), half(T.tm, t - 3, hh, 512), T.idn[:].indirect(half(T.txu, t, hh, 32)),
             ["idn", "txu%d" % t], ["tm%d_%d" % (t, hh)])

    step["t1r"] = lambda: act(T.t1r[:], T.st1[:].indirect(T.lb[:]), F.Copy, ["own1", "st1", "lb"], ["t1r"])
    step["h"] = lambda: tt(T.h[:], T.st1[:].indirect(T.la[:]), T.t1r[:], A.max, ["own1", "st1", "la", "t1r"], ["h"])

    def w3(row, src, key):
        before("y", [key, "w3a", "w3b"], [])
        Y.dma_start(T.w3[row::16, :], src).then_inc(T.sem.iw, 16)
        writer["w3_%d" % row] = [("iw", 32)]

    def g2():
        tolist(T.l2[:], T.n2[:], ["n2l"], ["l2"])
        cp(T.gt[:, 0:256].indirect(T.l2[:]), T.h[:], ["h", "l2"], ["g2"])

    step["w3"], step["w3n"], step["g2"] = lambda: w3(0, T.h[:], "h"), lambda: w3(1, T.n2r[:], "n2c"), g2
    step["n2l"] = lambda: act(T.n2[:], T.t1r[:, 0:16], F.Ln, ["t1r"], ["n2l"])
    step["ex"] = lambda: tt(T.ex[:], T.st1[:].indirect(T.jl[:, 0:16]), T.idr[:], A.mult,
                            ["own1", "st1", "jl0", "idr"], ["ex"])
    step["n2r"] = lambda: op("p", lambda: P.matmul(T.ph[:, 64:320], T.blk[:], T.ex[:], True, True), ["blk", "ex"],
                             ["ph", "n2r"])
    step["n2c"] = lambda: act(T.n2r[:], T.ph[:, 64:320], F.Copy, ["n2r"], ["ph", "n2c"])
    step["s2"] = lambda: copy("s2", T.xw[:], T.w3[:].indirect(T.w2u[:]), ["w3_0", "w3_1", "w2u"], ["xw"])
    step["fs2"] = lambda: fold("pe", 0, 64, "z0", lambda i: T.xw[:, i::16], ["xw"], "fs2")
    step["ls2"] = lambda: act(T.ls[:, 64:128], T.pe[:, 0:64], F.Ln, ["fs2"], ["pe", "ls2"])
    step["fs1"] = lambda: fold("ph", 0, 64, "z1", lambda i: T.xw[:, i::16], ["xw"], "fs1")
    step["ls1"] = lambda: act(T.ls[:, 0:64], T.ph[:, 0:64], F.Ln, ["fs1"], ["ph", "ls1"])
    step["off3"] = lambda: tolist(T.off[:, 0:64], T.ls[:, 64:128], ["ls2"], ["off3_0", "off3_1"])

    step["x4"] = lambda: tt(x4, T.h[:].indirect(T.lp[:]), mk4, A.mult, ["h", "lp", "mk4"], ["x4"])
    step["fx4"] = lambda: fold("pc", 32, 24, "z", lambda i: T.xf[:, M + i:2 * M:16], ["x4"], "fx4")
    step["f4"] = lambda: act(T.f4[:], T.pc[:, 32:56], F.Ln, ["fx4"], ["pc", "f4"])
    step["l4own"] = lambda: tolist(l4of(0), T.f4[:], ["f4"], ["l4_0"])
    step["sl4"] = lambda: send(l4of(0), ["l4_0"], off(peers, "al4"))
    step["xp"] = lambda: act(T.xp[:], x4.indirect(T.pru[:, 50:74]), F.Copy, ["x4", "pru"], ["xp"])
    step["fxp"] = lambda: fold("pd", 24, 24, "z", lambda i: T.xp[:, i::16], ["xp"], "fxp")
    step["fp"] = lambda: act(T.fp[:], T.pd[:, 24:48], F.Ln, ["fxp"], ["pd", "fp"])
    step["f4p"] = lambda: tolist(T.f4p[:], T.fp[:], ["fp"], ["f4p"])
    step["x5"] = lambda: tt(x5, T.gt[:, 0:C4].indirect(T.f4p[:]), mk5, A.mult, g23 + ["f4p", "mk5"], ["x5"])
    step["fx5"] = lambda: fold("pc", 64, 24, "z", lambda i: T.xf[:, 2 * M + i:3 * M:16], ["x5"], "fx5")
    step["f5"] = lambda: act(T.f5[:], T.pc[:, 64:88], F.Ln, ["fx5"], ["pc", "f5"])
    step["own5"] = lambda: tolist(l5of(r), T.f5[:], ["f5"], ["own5"])
    step["sl5"] = lambda: send(l5of(r), ["own5"], off(peers, "r5"), near(helpers[place], "h5", on_eng[:n_on // 2]),
                               near(mate, "q5", on_eng[n_on // 2:]))

    def under4(j):
        if "f" in var["sx4_%d" % j]:
            act(T.d4[:, M * j:M * (j + 1)], T.gt[:, 0:C4].indirect(l4of(j)), F.Copy, g23 + ["l4_%d" % j], ["d4_%d" % j])

    def part(base, d):
        def of(x):
            if "f" in var["sx%d_%d" % (d, x)]:
                return col(base, rank_of(x)), ["d4_%d" % x, "r4_%d" % x], [T.d4[:, M * x:M * (x + 1)], raw4(x)]
            return col(base, rank_of(x)), ["g%d_%d" % (d, x)], [col(base, rank_of(x))]
        return of

    def level5(j):
        q = rank_of(j) if j < 4 else 2 * order[j - 4] + 1 - place
        copy("l5_%d" % j, col(C5, q), T.gt[:, 0:C5].indirect(l5of(q)), g24 + ["own5", "l5own" if j < 4 else "l5in"],
             ["g5_%d" % j])

    for j in range(4):
        step["lc_%d" % j] = lambda j=j: cp(l3of(j), let3(j), ["c3_%d" % j], ["l3_%d" % j])
        step["lev3_%d" % j] = lambda j=j: tt(col(C3, rank_of(j)), T.h[:].indirect(l3of(j)), raw3(j), A.max,
                                             ["h", "l3_%d" % j, "r3_%d" % j], ["g3_%d" % j])
        step["lev4_%d" % j] = lambda j=j: tt(col(C4, rank_of(j)), T.gt[:, 0:C4].indirect(l4of(j)), raw4(j),
                                             A.max, g23 + ["l4_%d" % j, "r4_%d" % j], ["g4_%d" % j])
        step["d4_%d" % j] = lambda j=j: under4(j)
        step["sx3_%d" % j] = lambda j=j: pieces(3, j, part(C3, 3))
        step["sx4_%d" % j] = lambda j=j: pieces(4, j, part(C4, 4))
    for j in range(N):
        step["l5_%d" % j] = lambda j=j: level5(j)

    step["x3"] = lambda: act(x3, T.ex[:].indirect(l3of(0)), F.Copy, ["ex", "l3_0"], ["x3"])
    for d in range(3):
        step["fyf%d" % (d + 3)] = lambda d=d: fold("pg", 24 * d, 24, "z",
                                                   lambda i: T.xf[:, M * d + 24 * i:M * d + 24 * (i + 1)],
                                                   ["x%d" % (d + 3)], "fyf%d" % (d + 3))
    step["yg2"] = lambda: act(T.ygs[:, 2:34], T.gt[:, 32 * r:32 * r + 32], F.Ln, ["g2"], ["yg2"])
    step["yg3"] = lambda: act(T.ygs[:, 34:34 + M], col(C3, r), F.Ln, ["g3_0"], ["yg3"])
    step["yg4"] = lambda: act(T.ygs[:, 34 + M:802], col(C4, r), F.Ln, ["g4_0"], ["yg4"])
    step["yg5"] = lambda: act(T.ygs[:, 802:1186], col(C5, r), F.Ln, ["g5_0"], ["yg5"])

    def rnd(q, ap, rd, key):
        if q == "v":
            ts(ap, ap, K, MID + MAGIC, A.mult, A.add, rd, [key])
        else:
            act(ap, ap, F.Identity, rd, [key], bias=MID + MAGIC, scale=K)

    def sub(q, out, ap, rd, key):
        if q == "v":
            ts(out, ap, -MAGIC, None, A.add, None, rd, [key])
        else:
            act(out, ap, F.Identity, rd, [key], bias=-MAGIC)

    def yg_out(nm, a, b):
        sub(var["sb" + nm], T.ygs[:, a:b], T.ygs[:, a:b], ["rn" + nm], "sb" + nm)
        store("y", T.yg[:, a:b], T.ygs[:, a:b], ["sb" + nm, "x4in", "l5in"])

    for nm, a, b, rd in (("A", 0, 418, ["yg1", "yg2", "yg3"]), ("B", 418, 802, ["yg4"]), ("C", 802, 1186, ["yg5"])):
        step["rn" + nm] = lambda nm=nm, a=a, b=b, rd=rd: rnd(var["rn" + nm], T.ygs[:, a:b], rd, "rn" + nm)
        step["sb" + nm] = lambda nm=nm, a=a, b=b: yg_out(nm, a, b)

    def yfl():
        act(T.yfl[:], T.pg[:, 0:72], F.Ln, ["fyf3", "fyf4", "fyf5"], ["pg", "yfl0"])
        rnd(var["yfl"], T.yfl[:], ["yfl0"], "yfl1")
        sub(var["yfl"], T.yfl[:], T.yfl[:], ["yfl1"], "yfl")
        store("y", T.yf[:, 0:34], T.yf0[0::16, :], ["yf0a", "yf0b", "x4in", "l5in"])
        for d in range(3):
            store("y", T.yf[:, 34 + M * d:34 + M * (d + 1)], T.yfl[:, 24 * d:24 * d + 24], ["yfl"])

    step["yfl"] = yfl

    whole = lambda t: var["look%da" % t] == "F"
    bank_of = lambda t, hh: "pa" if (t % 2 if whole(t) else hh == 0) else "pb"

    def lsout(t, hh):
        return half(T.ol, hh, 0, 32) if t == 7 else half(T.ls, t - 1, hh, 32)

    def look(t, hh):
        top, keys = (C4, g23) if t == 3 else (C5, g24) if t == 4 else (CW, g25)
        if whole(t) and hh:
            return
        hs = [0, 1] if whole(t) else [hh]
        n, a = 32 * len(hs), 64 * (t - 3) + 32 * hh
        tt(T.xs[:, 16 * a:16 * (a + n)], T.gt[:, 0:top].indirect(T.off[:, a:a + n]), T.tm[:, 16 * a:16 * (a + n)],
           A.mult, keys + ["off%d_%d" % (t, x) for x in hs] + ["tm%d_%d" % (t, x) for x in hs], ["x%d_%d" % (t, hh)])
        fold(bank_of(t, hh), a, n, "z", lambda i: T.xs[:, 16 * a + i:16 * (a + n):16], ["x%d_%d" % (t, hh)],
             "fx%d_%d" % (t, hh))

    def ln(t, hh):
        bank, a = bank_of(t, hh), 64 * (t - 3)
        if whole(t) and t != 7:
            if hh == 0:
                act(T.ls[:, 64 * (t - 1):64 * t], T[bank][:, a:a + 64], F.Ln, ["fx%d_0" % t],
                    [bank, "ls%d_0" % t, "ls%d_1" % t])
            return
        act(lsout(t, hh), T[bank][:, a + 32 * hh:a + 32 * hh + 32], F.Ln, ["fx%d_%d" % (t, 0 if whole(t) else hh)],
            [bank, "ls%d_%d" % (t, hh)])

    def nxt(t, hh):
        u = t - 1
        if whole(u):
            if hh == 0:
                tolist(T.off[:, 64 * (t - 3):64 * (t - 2)], T.ls[:, 64 * (u - 1):64 * u], ["ls%d_0" % u, "ls%d_1" % u],
                       ["off%d_0" % t, "off%d_1" % t])
            return
        tolist(half(T.off, t - 3, hh, 32), lsout(u, hh), ["ls%d_%d" % (u, hh)], ["off%d_%d" % (t, hh)])

    def most(t):
        tt(T.mx[:], T.mx[:], T.ls[:, 64 * (t - 1):64 * t], A.max, ["mx0", "ls%d_0" % t, "ls%d_1" % t],
           ["mx", "mx%d" % t])

    def mx():
        tt(T.mx[:], T.ls[:, 0:64], T.ls[:, 64:128], A.max, ["ls1", "ls2"], ["mx0", "mx"])
        most(3)

    def end(hh):
        tt(half(T.ol, hh, 1, 32), half(T.mx, 0, hh, 32), half(T.ol, hh, 0, 32), A.max,
           ["mx", "mx4", "mx5", "mx6", "ls7_%d" % hh], ["ol0_%d" % hh])
        rnd("v", T.ol[:, 64 * hh:64 * hh + 64], ["ol0_%d" % hh], "ol1_%d" % hh)
        sub("v", half(T.oo, 0, hh, 32), half(T.ol, hh, 0, 32), ["ol1_%d" % hh], "ol2_%d" % hh)
        sub("a", half(T.oo, 1, hh, 32), half(T.ol, hh, 1, 32), ["ol1_%d" % hh], "ol3_%d" % hh)

    def end_b():
        end(1)
        store("y", T.yl[:], T.oo[:, 0:64], ["ol2_0", "ol2_1"])
        store("a", T.ym[:], T.oo[:, 64:128], ["ol3_0", "ol3_1"])

    for t in range(3, 8):
        for hh in range(2):
            for name, fn in (("tm", tmask), ("look", look), ("ln", ln), ("nxt", nxt)):
                step["%s%d%s" % (name, t, "ab"[hh])] = lambda fn=fn, t=t, hh=hh: fn(t, hh)
        step["most%d" % t] = lambda t=t: most(t)
    step["mx"], step["enda"], step["endb"] = mx, lambda: end(0), end_b

    for name in ORDER:
        step[name.partition(":")[0]]()

    wait("g", [("loc", loc[0])])
    wait("y", [("sv", count["v"]), ("sa", count["a"]), ("sp", count["p"]), ("sg", count["g"]), ("out", outs[0])])
